import numpy as np
import ml_dtypes


def mxq(x, axis, fmt="e4m3"):
    dtype, down = {"e4m3": (ml_dtypes.float8_e4m3fn, 7), "e5m2": (ml_dtypes.float8_e5m2, 14)}[fmt]
    v = np.moveaxis(np.asarray(x, np.float32).astype(ml_dtypes.bfloat16).astype(np.float64), axis, -1)
    blocks = v.reshape(v.shape[:-1] + (-1, 32))
    amax = np.abs(blocks).max(-1, keepdims=True)
    byte = np.maximum(np.where(amax > 0, np.frexp(amax)[1] - 1 + 127, 0) - down, 1)
    scale = np.exp2(byte - 127.0)
    codes = (blocks / scale).astype(np.float32).astype(dtype).astype(np.float64)
    return np.moveaxis((codes * scale).reshape(v.shape), -1, axis)


WIDE = False


def mx_kscale(k):
    if not WIDE:
        return np.ones(k)
    levels = np.array([10, -10, 5, -5, 0])
    if k % 512:
        return np.exp2(np.random.permutation(np.resize(levels, k // 32))).repeat(32)
    a = np.empty((k // 512, 16))
    for p in range(k // 512):
        a[p, :8] = np.random.permutation(np.resize(levels, 8))
        for g in range(8):
            far = levels[np.abs(levels - a[p, g]) >= 10]
            a[p, g + 8] = far[np.random.randint(len(far))]
    return np.exp2(a.ravel()).repeat(32)


def f64(x):
    return np.asarray(x).astype(np.float64)


def striped(idx):
    return np.tile(idx.reshape(-1, 16).T, (8, 1)).astype(np.uint16)


def unstriped(offs):
    return offs[:16].T.reshape(-1).astype(np.int64)


def striped8(idx):
    return np.concatenate([x.reshape(-1, 16).T for x in idx]).astype(np.uint16)


def runs(offs, k):
    lists = np.stack([offs[16 * r : 16 * r + 16].T.reshape(-1) for r in range(8)]).astype(np.int64)
    return lists[np.arange(k) % 512 // 64]


def pack_weight(w):
    k, n = w.shape
    w = f64(np.asarray(w, np.float32).astype(ml_dtypes.bfloat16)).reshape(k // 32, 32, n)
    amax = np.abs(w).max(1)
    byte = np.clip(np.where(amax > 0, np.frexp(amax)[1] - 1 + 127 - 7, 1), 1, 254)
    scaled = (w * np.exp2(127.0 - byte)[:, None, :]).reshape(k, n).astype(np.float32)
    words = np.ascontiguousarray(scaled.reshape(k // 512, 128, 4, n).transpose(0, 1, 3, 2)).astype(ml_dtypes.float8_e4m3fn).view(np.uint8)
    return words, np.ascontiguousarray(byte.astype(np.uint8).reshape(k // 512, 16, n))


def unpack_weight(words, scales):
    g, p, n, _ = words.shape
    vals = np.ascontiguousarray(words).view(ml_dtypes.float8_e4m3fn).astype(np.float64) * np.repeat(np.exp2(scales.astype(np.float64) - 127.0), 8, axis=1)[..., None]
    return vals.transpose(0, 1, 3, 2).reshape(g * 512, n)


def sigmoid(v):
    return 1.0 / (1.0 + np.exp(-np.maximum(v, -700.0)))


K, T, S, N, H = 512, 2048, 512, 512, 512


def setup_inputs():
    n = np.random.standard_normal
    s = mx_kscale(K)[:, None]
    u = mx_kscale(H)
    packed_xT = pack_weight(n((K, T)) * s)
    return {
        "x_words": packed_xT[0],
        "x_scales": packed_xT[1],
        "w1": (n((K, H)) / np.sqrt(K) / s).astype(np.float32),
        "w2": (n((K, H)) / np.sqrt(K) / s * u).astype(np.float32),
        "w3": (n((H, N)) / np.sqrt(H) / u[:, None]).astype(np.float32),
        "offs": striped(np.random.permutation(T)[:S]),
        "near": striped8(np.random.randint(0, S, (8, S))),
        "far": striped8(np.random.randint(0, S, (8, S))),
    }


def reference(x_words, x_scales, w1, w2, w3, offs, near, far):
    xq = unpack_weight(x_words, x_scales)[:, unstriped(offs)]
    b = mxq(f64(w2), 0, "e4m3").T @ xq
    a = sigmoid(mxq(f64(w1), 0, "e4m3").T @ xq)
    b2 = b + a * (b[np.arange(H)[:, None], runs(near, H)])
    a2 = a * (a[np.arange(H)[:, None], runs(near, H)])
    z = b2 + a2 * (b2[np.arange(H)[:, None], runs(far, H)])
    return mxq(f64(w3), 0, "e4m3").T @ mxq(z, 0, "e4m3")

@@ -1,0 +1,214 @@
+from contextlib import ExitStack
+
+import concourse.mybir as mybir
+
+K, T, S, H, N = 512, 2048, 512, 512, 512
+FLOPS = 2 * K * H * S * 2 + 2 * H * N * S
+
+F32 = mybir.dt.float32
+BF16 = mybir.dt.bfloat16
+I32 = mybir.dt.int32
+U32 = mybir.dt.uint32
+U16 = mybir.dt.uint16
+U8 = mybir.dt.uint8
+FP8X4 = mybir.dt.float8_e4m3fn_x4
+MULT = mybir.AluOpType.mult
+ADD = mybir.AluOpType.add
+SIGMOID = mybir.ActivationFunctionType.Sigmoid
+
+P = 128
+PACK = 4
+HALF = 256
+FAR_CHUNKS = ((0, 256), (256, 512))
+W1_VECTOR_M = 42
+
+
+def tile_picked_scan2_none_p_kernel(
+    tc, x_words, x_scales, w1, w2, w3, offs, near, far, out
+):
+    nc = tc.nc
+    with ExitStack() as ctx:
+        keep = ctx.enter_context(tc.tile_pool(name="keep", bufs=1))
+        psum = ctx.enter_context(tc.psum_pool(name="psum", bufs=1))
+
+        def tiles(name, shape, dtype, n):
+            return [keep.tile(shape, dtype, name="%s%d" % (name, i), align_bytes=64) for i in range(n)]
+
+        offs_sb = keep.tile([P, S // 16], U16, name="offs_sb")
+        near_sb = keep.tile([P, S // 16], U16, name="near_sb")
+        far_sb = keep.tile([P, S // 16], U16, name="far_sb")
+        xw = keep.tile([P, T], I32, name="xw", align_bytes=64)
+        xs = keep.tile([P, T], U8, name="xs", align_bytes=64)
+        xw_pick = keep.tile([P, S], U32, name="xw_pick", align_bytes=64)
+        xs_pick = keep.tile([P, S], U8, name="xs_pick", align_bytes=64)
+        warm = keep.tile([P, 2], F32, name="warm")
+
+        w1_raw = tiles("w1_raw", [P, PACK, HALF], F32, 2)
+        w2_raw = tiles("w2_raw", [P, PACK, HALF], F32, 2)
+        w3_raw = tiles("w3_raw", [P, PACK, HALF], F32, 2)
+        w_bf = tiles("w_bf", [P, PACK * H], BF16, 3)
+        w_codes = tiles("w_codes", [P, H], U32, 3)
+        w_scales = tiles("w_scales", [P, H], U8, 3)
+
+        u_sb = tiles("u", [P, S], F32, PACK)
+        a_sb = tiles("a", [P, S], F32, PACK)
+        an_sb = tiles("an", [P, S], F32, PACK)
+        a2_sb = tiles("a2", [P, S], F32, PACK)
+        b_sb = tiles("b", [P, S], F32, PACK)
+        g1_sb = tiles("g1", [P, S], F32, PACK)
+        b2_sb = tiles("b2", [P, S], F32, PACK)
+        b2_all = keep.tile([P, PACK, S], F32, name="b2_all", align_bytes=64)
+        g2_all = keep.tile([P, PACK, S], F32, name="g2_all", align_bytes=64)
+        z_bf = keep.tile([P, PACK * S], BF16, name="z_bf", align_bytes=64)
+        z_codes = keep.tile([P, S], U32, name="z_codes", align_bytes=64)
+        z_scales = keep.tile([P, S], U8, name="z_scales", align_bytes=64)
+
+        def load_weight(w, raw):
+            rows = w.rearrange("(p j) c -> p j c", j=PACK)
+            for h in range(2):
+                nc.sync.dma_start(out=raw[h][:], in_=rows[:, :, h * HALF : (h + 1) * HALF])
+
+        nc.vector.memset(xs[:].bitcast(I32), 0)
+        nc.sync.dma_start(offs_sb[:], offs)
+        nc.sync.dma_start(out=xw[:], in_=x_words[0].rearrange("p n t -> p (n t)").bitcast(I32))
+        for q in range(4):
+            nc.scalar.dma_start(
+                out=xs[32 * q : 32 * q + 4, :].bitcast(I32), in_=x_scales[0, 4 * q : 4 * q + 4, :].bitcast(I32)
+            )
+        nc.gpsimd.memset(warm[:, 0:1], 0.0)
+        nc.scalar.activation(warm[:, 1:2], warm[:, 0:1], SIGMOID)
+        load_weight(w1, w1_raw)
+        nc.sync.dma_start(near_sb[:], near)
+        load_weight(w2, w2_raw)
+        nc.sync.dma_start(far_sb[:], far)
+        load_weight(w3, w3_raw)
+
+        nc.vector.tensor_copy(xs_pick[:], xs[:].indirect(offs_sb[:]))
+        nc.vector.tensor_copy(xw_pick[:], xw[:].bitcast(U32).indirect(offs_sb[:]))
+
+        def cast_dealt(copy, i, raw, h, m0, m1):
+            dst = w_bf[i][:].rearrange("p (t m j) -> p m j t", t=PACK, j=PACK)
+            src = raw[h][:].rearrange("p j (m t) -> p m j t", t=PACK)
+            copy(dst[:, 64 * h + m0 : 64 * h + m1], src[:, m0:m1])
+
+        def quantize(i, c0, c1):
+            nc.vector.quantize_mx(
+                out=w_codes[i][:, c0:c1].bitcast(FP8X4),
+                scales=w_scales[i][:, c0:c1],
+                in_=w_bf[i][:, PACK * c0 : PACK * c1],
+            )
+
+        def first_product(i, t, name):
+            acc = psum.tile([P, S], F32, name=name)
+            cols = slice(P * t, P * (t + 1))
+            nc.tensor.matmul_mx(
+                out=acc[:],
+                lhsT=w_codes[i][:, cols].bitcast(FP8X4),
+                lhsT_scale=w_scales[i][:, cols],
+                rhs=xw_pick[:].bitcast(FP8X4),
+                rhs_scale=xs_pick[:],
+                start=True,
+                stop=True,
+            )
+            return acc
+
+        def halves(lists):
+            return [(slice(h * HALF, (h + 1) * HALF), lists[:, 16 * h : 16 * (h + 1)]) for h in range(2)]
+
+        for h in range(2):
+            cast_dealt(nc.vector.tensor_copy, 0, w1_raw, h, 0, W1_VECTOR_M)
+            cast_dealt(nc.scalar.copy, 0, w1_raw, h, W1_VECTOR_M, 64)
+        for t in range(PACK):
+            quantize(0, P * t, P * (t + 1))
+        u_ps = [first_product(0, t, "bank%d" % t) for t in range(PACK)]
+        for h in range(2):
+            cast_dealt(nc.vector.tensor_copy, 1, w2_raw, h, 0, 64)
+        for t in range(PACK):
+            quantize(1, P * t, P * (t + 1))
+        b_ps = [first_product(1, t, "bank%d" % (PACK + t)) for t in range(PACK)]
+
+        def decay(t):
+            nc.scalar.activation(a_sb[t][:], u_ps[t][:], SIGMOID)
+
+        def decay_near(t):
+            nc.scalar.copy(u_sb[t][:], u_ps[t][:])
+            for cols, lst in halves(near_sb):
+                nc.scalar.activation(an_sb[t][:, cols], u_sb[t][:].indirect(lst), SIGMOID)
+
+        def carry_near(t):
+            for cols, lst in halves(near_sb):
+                nc.vector.tensor_tensor(g1_sb[t][:, cols], b_sb[t][:].indirect(lst), a_sb[t][:, cols], MULT)
+
+        def first_step(t):
+            nc.vector.tensor_tensor(b2_sb[t][:], g1_sb[t][:], b_sb[t][:], ADD)
+            nc.vector.tensor_tensor(a2_sb[t][:], a_sb[t][:], an_sb[t][:], MULT)
+
+        decay(0)
+        decay_near(0)
+        decay(1)
+        for t in range(PACK):
+            nc.scalar.copy(b_sb[t][:], b_ps[t][:])
+            carry_near(t)
+            if t >= 1:
+                first_step(t - 1)
+            if t + 2 < PACK:
+                decay(t + 2)
+            if t + 1 < PACK:
+                decay_near(t + 1)
+        first_step(PACK - 1)
+        for t in range(PACK):
+            nc.scalar.copy(b2_all[:, t, :], b2_sb[t][:])
+
+        for h in range(2):
+            dst = w_bf[2][:, 4 * HALF * h : 4 * HALF * (h + 1)].rearrange("p (c i j) -> p c j i", i=2, j=PACK)
+            nc.scalar.copy(dst, w3_raw[h][:].rearrange("p j (c i) -> p c j i", i=2))
+
+        out_rows = out.rearrange("(r p) s -> p r s", p=P)
+
+        def carry_far(c0, c1):
+            for t in range(PACK):
+                nc.vector.tensor_tensor(
+                    g2_all[:, t, c0:c1], b2_sb[t][:].indirect(far_sb[:, c0 // 16 : c1 // 16]), a2_sb[t][:, c0:c1], MULT
+                )
+
+        def second_step(c0, c1):
+            nc.vector.tensor_tensor(
+                z_bf[:, PACK * c0 : PACK * c1].rearrange("p (c i t) -> p c t i", i=2, t=PACK),
+                g2_all[:, :, c0:c1].rearrange("p t (c i) -> p c t i", i=2),
+                b2_all[:, :, c0:c1].rearrange("p t (c i) -> p c t i", i=2),
+                ADD,
+            )
+
+        def last_product(n, c0, c1):
+            nc.vector.quantize_mx(
+                out=z_codes[:, c0:c1].bitcast(FP8X4), scales=z_scales[:, c0:c1], in_=z_bf[:, PACK * c0 : PACK * c1]
+            )
+            res = keep.tile([P, PACK, c1 - c0], F32, name="res%d" % n)
+            for pair in range(2):
+                acc = psum.tile([P, 2, c1 - c0], F32, name="bank%d" % (2 * n + pair))
+                for r in range(2):
+                    cols = slice(P * (2 * pair + r), P * (2 * pair + r + 1))
+                    nc.tensor.matmul_mx(
+                        out=acc[:, r, :],
+                        lhsT=w_codes[2][:, cols].bitcast(FP8X4),
+                        lhsT_scale=w_scales[2][:, cols],
+                        rhs=z_codes[:, c0:c1].bitcast(FP8X4),
+                        rhs_scale=z_scales[:, c0:c1],
+                        start=True,
+                        stop=True,
+                    )
+                rows = slice(2 * pair, 2 * pair + 2)
+                if pair == 1 and c1 == S:
+                    nc.vector.tensor_copy(res[:, rows, :], acc[:])
+                else:
+                    nc.scalar.copy(res[:, rows, :], acc[:])
+                nc.sync.dma_start(out=out_rows[:, rows, c0:c1], in_=res[:, rows, :])
+
+        for n, (c0, c1) in enumerate(FAR_CHUNKS):
+            carry_far(c0, c1)
+            if n == 0:
+                quantize(2, 0, N)
+            else:
+                last_product(n - 1, *FAR_CHUNKS[n - 1])
+            second_step(c0, c1)
+        last_product(len(FAR_CHUNKS) - 1, *FAR_CHUNKS[-1])

@@ -19,8 +19,8 @@ SIGMOID = mybir.ActivationFunctionType.Sigmoid
 P = 128
 PACK = 4
 HALF = 256
-FAR_CHUNKS = ((0, 256), (256, 512))
-W1_VECTOR_M = 42
+FAR_CHUNKS = ((0, 384), (384, 512))
+OUT_CHUNKS = ((0, 256), (256, 384), (384, 512))
 
 
 def tile_picked_scan2_none_p_kernel(
@@ -31,72 +31,64 @@ def tile_picked_scan2_none_p_kernel(
         keep = ctx.enter_context(tc.tile_pool(name="keep", bufs=1))
         psum = ctx.enter_context(tc.psum_pool(name="psum", bufs=1))
 
+        def tile(name, shape, dtype):
+            return keep.tile(shape, dtype, name=name, align_bytes=64)
+
         def tiles(name, shape, dtype, n):
-            return [keep.tile(shape, dtype, name="%s%d" % (name, i), align_bytes=64) for i in range(n)]
+            return [tile("%s%d" % (name, i), shape, dtype) for i in range(n)]
 
         offs_sb = keep.tile([P, S // 16], U16, name="offs_sb")
         near_sb = keep.tile([P, S // 16], U16, name="near_sb")
         far_sb = keep.tile([P, S // 16], U16, name="far_sb")
-        xw = keep.tile([P, T], I32, name="xw", align_bytes=64)
-        xs = keep.tile([P, T], U8, name="xs", align_bytes=64)
-        xw_pick = keep.tile([P, S], U32, name="xw_pick", align_bytes=64)
-        xs_pick = keep.tile([P, S], U8, name="xs_pick", align_bytes=64)
+        xw = tile("xw", [P, T], I32)
+        xs = tile("xs", [P, T], U8)
+        xw_pick = tile("xw_pick", [P, S], U32)
+        xs_pick = tile("xs_pick", [P, S], U8)
         warm = keep.tile([P, 2], F32, name="warm")
 
-        w1_raw = tiles("w1_raw", [P, PACK, HALF], F32, 2)
-        w2_raw = tiles("w2_raw", [P, PACK, HALF], F32, 2)
-        w3_raw = tiles("w3_raw", [P, PACK, HALF], F32, 2)
-        w_bf = tiles("w_bf", [P, PACK * H], BF16, 3)
+        w_raw = tiles("w_raw", [P, PACK, H], F32, 3)
         w_codes = tiles("w_codes", [P, H], U32, 3)
         w_scales = tiles("w_scales", [P, H], U8, 3)
 
-        u_sb = tiles("u", [P, S], F32, PACK)
-        a_sb = tiles("a", [P, S], F32, PACK)
+        ba_sb = tiles("ba", [P, 2 * S], F32, PACK)
+        b_sb = [ba_sb[t][:, 0:S] for t in range(PACK)]
+        a_sb = [ba_sb[t ^ 1][:, S : 2 * S] for t in range(PACK)]
         an_sb = tiles("an", [P, S], F32, PACK)
-        a2_sb = tiles("a2", [P, S], F32, PACK)
-        b_sb = tiles("b", [P, S], F32, PACK)
         g1_sb = tiles("g1", [P, S], F32, PACK)
         b2_sb = tiles("b2", [P, S], F32, PACK)
-        b2_all = keep.tile([P, PACK, S], F32, name="b2_all", align_bytes=64)
-        g2_all = keep.tile([P, PACK, S], F32, name="g2_all", align_bytes=64)
-        z_bf = keep.tile([P, PACK * S], BF16, name="z_bf", align_bytes=64)
-        z_codes = keep.tile([P, S], U32, name="z_codes", align_bytes=64)
-        z_scales = keep.tile([P, S], U8, name="z_scales", align_bytes=64)
+        b2_all = tile("b2_all", [P, PACK, S], F32)
+        g2_all = tile("g2_all", [P, PACK, 384], F32)
+        z_bf = tile("z_bf", [P, PACK * S], BF16)
+        z_codes = tile("z_codes", [P, S], U32)
+        z_scales = tile("z_scales", [P, S], U8)
 
-        def load_weight(w, raw):
-            rows = w.rearrange("(p j) c -> p j c", j=PACK)
-            for h in range(2):
-                nc.sync.dma_start(out=raw[h][:], in_=rows[:, :, h * HALF : (h + 1) * HALF])
+        def load_weight(i, w):
+            nc.sync.dma_start(out=w_raw[i][:], in_=w.rearrange("(p j) c -> p j c", j=PACK))
 
-        nc.vector.memset(xs[:].bitcast(I32), 0)
+        nc.gpsimd.memset(xs[:].bitcast(I32), 0)
         nc.sync.dma_start(offs_sb[:], offs)
         nc.sync.dma_start(out=xw[:], in_=x_words[0].rearrange("p n t -> p (n t)").bitcast(I32))
         for q in range(4):
-            nc.scalar.dma_start(
+            nc.sync.dma_start(
                 out=xs[32 * q : 32 * q + 4, :].bitcast(I32), in_=x_scales[0, 4 * q : 4 * q + 4, :].bitcast(I32)
             )
+        load_weight(0, w1)
         nc.gpsimd.memset(warm[:, 0:1], 0.0)
         nc.scalar.activation(warm[:, 1:2], warm[:, 0:1], SIGMOID)
-        load_weight(w1, w1_raw)
         nc.sync.dma_start(near_sb[:], near)
-        load_weight(w2, w2_raw)
+        load_weight(1, w2)
         nc.sync.dma_start(far_sb[:], far)
-        load_weight(w3, w3_raw)
+        load_weight(2, w3)
 
-        nc.vector.tensor_copy(xs_pick[:], xs[:].indirect(offs_sb[:]))
-        nc.vector.tensor_copy(xw_pick[:], xw[:].bitcast(U32).indirect(offs_sb[:]))
+        def cast_dealt(copy, i, t0, tag):
+            values = tile(tag, [P, 2 * H], BF16)
+            dst = values[:].rearrange("p (t m j) -> p m j t", t=2, j=PACK)
+            src = w_raw[i][:].rearrange("p j (m t) -> p m j t", t=PACK)
+            copy(dst, src[:, :, :, t0 : t0 + 2])
+            return values
 
-        def cast_dealt(copy, i, raw, h, m0, m1):
-            dst = w_bf[i][:].rearrange("p (t m j) -> p m j t", t=PACK, j=PACK)
-            src = raw[h][:].rearrange("p j (m t) -> p m j t", t=PACK)
-            copy(dst[:, 64 * h + m0 : 64 * h + m1], src[:, m0:m1])
-
-        def quantize(i, c0, c1):
-            nc.vector.quantize_mx(
-                out=w_codes[i][:, c0:c1].bitcast(FP8X4),
-                scales=w_scales[i][:, c0:c1],
-                in_=w_bf[i][:, PACK * c0 : PACK * c1],
-            )
+        def quantize(codes, scales, c0, c1, values):
+            nc.vector.quantize_mx(out=codes[:, c0:c1].bitcast(FP8X4), scales=scales[:, c0:c1], in_=values)
 
         def first_product(i, t, name):
             acc = psum.tile([P, S], F32, name=name)
@@ -112,80 +104,95 @@ def tile_picked_scan2_none_p_kernel(
             )
             return acc
 
-        def halves(lists):
-            return [(slice(h * HALF, (h + 1) * HALF), lists[:, 16 * h : 16 * (h + 1)]) for h in range(2)]
-
-        for h in range(2):
-            cast_dealt(nc.vector.tensor_copy, 0, w1_raw, h, 0, W1_VECTOR_M)
-            cast_dealt(nc.scalar.copy, 0, w1_raw, h, W1_VECTOR_M, 64)
-        for t in range(PACK):
-            quantize(0, P * t, P * (t + 1))
-        u_ps = [first_product(0, t, "bank%d" % t) for t in range(PACK)]
-        for h in range(2):
-            cast_dealt(nc.vector.tensor_copy, 1, w2_raw, h, 0, 64)
-        for t in range(PACK):
-            quantize(1, P * t, P * (t + 1))
-        b_ps = [first_product(1, t, "bank%d" % (PACK + t)) for t in range(PACK)]
+        nc.vector.tensor_copy(xw_pick[:], xw[:].bitcast(U32).indirect(offs_sb[:]))
+        nc.vector.tensor_copy(xs_pick[:], xs[:].indirect(offs_sb[:]))
+        w1_low = cast_dealt(nc.vector.tensor_copy, 0, 0, "w1_low")
+        w1_high = cast_dealt(nc.scalar.copy, 0, 2, "w1_high")
+        quantize(w_codes[0], w_scales[0], 0, 2 * P, w1_low[:])
+        quantize(w_codes[0], w_scales[0], 2 * P, 4 * P, w1_high[:])
+        u_ps = [first_product(0, t, "bank%d" % t) for t in range(PACK - 1)]
+        w2_low = cast_dealt(nc.vector.tensor_copy, 1, 0, "w2_pair")
+        quantize(w_codes[1], w_scales[1], 0, P, w2_low[:, 0:H])
+        quantize(w_codes[1], w_scales[1], P, 2 * P, w2_low[:, H : 2 * H])
+        w2_high = cast_dealt(nc.vector.tensor_copy, 1, 2, "w2_pair")
+        quantize(w_codes[1], w_scales[1], 2 * P, 4 * P, w2_high[:])
+        b_ps = [first_product(1, t, "bank%d" % (PACK - 1 + t)) for t in range(2)]
+        a2_sb = g1_sb
 
         def decay(t):
-            nc.scalar.activation(a_sb[t][:], u_ps[t][:], SIGMOID)
+            nc.scalar.activation(a_sb[t], u_ps[t][:], SIGMOID)
 
-        def decay_near(t):
-            nc.scalar.copy(u_sb[t][:], u_ps[t][:])
-            for cols, lst in halves(near_sb):
-                nc.scalar.activation(an_sb[t][:, cols], u_sb[t][:].indirect(lst), SIGMOID)
+        def decay_near(t, tag):
+            u_sb = tile(tag, [P, S], F32)
+            nc.scalar.copy(u_sb[:], u_ps[t][:])
+            for h in range(2):
+                lst = near_sb[:, 16 * h : 16 * (h + 1)]
+                nc.scalar.activation(an_sb[t][:, HALF * h : HALF * (h + 1)], u_sb[:].indirect(lst), SIGMOID)
+
+        def carry_in(t):
+            nc.scalar.copy(b_sb[t], b_ps[t][:])
 
         def carry_near(t):
-            for cols, lst in halves(near_sb):
-                nc.vector.tensor_tensor(g1_sb[t][:, cols], b_sb[t][:].indirect(lst), a_sb[t][:, cols], MULT)
+            nc.vector.tensor_tensor(g1_sb[t][:], ba_sb[t][:].indirect(near_sb[:]), a_sb[t], MULT)
 
         def first_step(t):
-            nc.vector.tensor_tensor(b2_sb[t][:], g1_sb[t][:], b_sb[t][:], ADD)
-            nc.vector.tensor_tensor(a2_sb[t][:], a_sb[t][:], an_sb[t][:], MULT)
+            nc.vector.tensor_tensor(b2_sb[t][:], g1_sb[t][:], b_sb[t], ADD)
 
-        decay(0)
-        decay_near(0)
-        decay(1)
+        def decay_product(t):
+            nc.vector.tensor_tensor(a2_sb[t][:], a_sb[t], an_sb[t][:], MULT)
+
+        for t in range(PACK - 1):
+            decay(t)
+        carry_in(0)
+        u_ps.append(first_product(0, 3, "bank3"))
+        b_ps.extend(first_product(1, t, "bank%d" % (PACK - 1 + t)) for t in range(2, PACK))
+        carry_in(1)
+        decay(3)
+        carry_in(2)
+        carry_in(3)
         for t in range(PACK):
-            nc.scalar.copy(b_sb[t][:], b_ps[t][:])
-            carry_near(t)
-            if t >= 1:
-                first_step(t - 1)
-            if t + 2 < PACK:
-                decay(t + 2)
-            if t + 1 < PACK:
-                decay_near(t + 1)
-        first_step(PACK - 1)
+            decay_near(t, "w_codes1" if t % 2 == 0 else "w_scales1")
+        carry_near(0)
+        carry_near(1)
+        first_step(0)
+        carry_near(2)
+        first_step(1)
+        decay_product(0)
+        carry_near(3)
+        first_step(2)
+        decay_product(1)
+        first_step(3)
+        decay_product(2)
+        decay_product(3)
         for t in range(PACK):
             nc.scalar.copy(b2_all[:, t, :], b2_sb[t][:])
-
-        for h in range(2):
-            dst = w_bf[2][:, 4 * HALF * h : 4 * HALF * (h + 1)].rearrange("p (c i j) -> p c j i", i=2, j=PACK)
-            nc.scalar.copy(dst, w3_raw[h][:].rearrange("p j (c i) -> p c j i", i=2))
+        w3_bf = tile("w_scales1", [P, PACK * N], BF16)
+        nc.scalar.copy(
+            w3_bf[:].rearrange("p (c i j) -> p c j i", i=2, j=PACK), w_raw[2][:].rearrange("p j (c i) -> p c j i", i=2)
+        )
 
         out_rows = out.rearrange("(r p) s -> p r s", p=P)
 
-        def carry_far(c0, c1):
+        def carry_far(c0, c1, g0):
             for t in range(PACK):
                 nc.vector.tensor_tensor(
-                    g2_all[:, t, c0:c1], b2_sb[t][:].indirect(far_sb[:, c0 // 16 : c1 // 16]), a2_sb[t][:, c0:c1], MULT
+                    g2_all[:, t, g0 : g0 + c1 - c0], b2_sb[t][:].indirect(far_sb[:, c0 // 16 : c1 // 16]), a2_sb[t][:, c0:c1], MULT
                 )
 
-        def second_step(c0, c1):
+        def second_step(c0, c1, g0):
             nc.vector.tensor_tensor(
                 z_bf[:, PACK * c0 : PACK * c1].rearrange("p (c i t) -> p c t i", i=2, t=PACK),
-                g2_all[:, :, c0:c1].rearrange("p t (c i) -> p c t i", i=2),
+                g2_all[:, :, g0 : g0 + c1 - c0].rearrange("p t (c i) -> p c t i", i=2),
                 b2_all[:, :, c0:c1].rearrange("p t (c i) -> p c t i", i=2),
                 ADD,
             )
 
-        def last_product(n, c0, c1):
-            nc.vector.quantize_mx(
-                out=z_codes[:, c0:c1].bitcast(FP8X4), scales=z_scales[:, c0:c1], in_=z_bf[:, PACK * c0 : PACK * c1]
-            )
+        def last_product(n):
+            c0, c1 = OUT_CHUNKS[n]
+            quantize(z_codes, z_scales, c0, c1, z_bf[:, PACK * c0 : PACK * c1])
             res = keep.tile([P, PACK, c1 - c0], F32, name="res%d" % n)
             for pair in range(2):
-                acc = psum.tile([P, 2, c1 - c0], F32, name="bank%d" % (2 * n + pair))
+                acc = psum.tile([P, 2, c1 - c0], F32, name="bank%d" % ((4 + 2 * n + pair) % 8))
                 for r in range(2):
                     cols = slice(P * (2 * pair + r), P * (2 * pair + r + 1))
                     nc.tensor.matmul_mx(
@@ -202,13 +209,15 @@ def tile_picked_scan2_none_p_kernel(
                     nc.vector.tensor_copy(res[:, rows, :], acc[:])
                 else:
                     nc.scalar.copy(res[:, rows, :], acc[:])
-                nc.sync.dma_start(out=out_rows[:, rows, c0:c1], in_=res[:, rows, :])
+                queue = nc.scalar if pair == 0 and c1 == S else nc.sync
+                queue.dma_start(out=out_rows[:, rows, c0:c1], in_=res[:, rows, :])
 
-        for n, (c0, c1) in enumerate(FAR_CHUNKS):
-            carry_far(c0, c1)
-            if n == 0:
-                quantize(2, 0, N)
-            else:
-                last_product(n - 1, *FAR_CHUNKS[n - 1])
-            second_step(c0, c1)
-        last_product(len(FAR_CHUNKS) - 1, *FAR_CHUNKS[-1])
+        carry_far(0, 384, 0)
+        second_step(0, 256, 0)
+        second_step(256, 384, 256)
+        quantize(w_codes[2], w_scales[2], 0, N, w3_bf[:])
+        last_product(0)
+        carry_far(384, 512, 0)
+        last_product(1)
+        second_step(384, 512, 0)
+        last_product(2)

@@ -18,9 +18,10 @@ SIGMOID = mybir.ActivationFunctionType.Sigmoid
 
 P = 128
 PACK = 4
+GROUP = 16
 HALF = 256
-FAR_CHUNKS = ((0, 384), (384, 512))
-OUT_CHUNKS = ((0, 256), (256, 384), (384, 512))
+TAIL = S - P
+OUT_CHUNKS = ((0, HALF), (HALF, TAIL), (TAIL, S))
 
 
 def tile_picked_scan2_none_p_kernel(
@@ -34,158 +35,159 @@ def tile_picked_scan2_none_p_kernel(
         def tile(name, shape, dtype):
             return keep.tile(shape, dtype, name=name, align_bytes=64)
 
-        def tiles(name, shape, dtype, n):
-            return [tile("%s%d" % (name, i), shape, dtype) for i in range(n)]
+        def tiles(name, shape, dtype, count):
+            return [tile("%s%d" % (name, i), shape, dtype) for i in range(count)]
 
-        offs_sb = keep.tile([P, S // 16], U16, name="offs_sb")
-        near_sb = keep.tile([P, S // 16], U16, name="near_sb")
-        far_sb = keep.tile([P, S // 16], U16, name="far_sb")
+        offs_sb = keep.tile([P, S // GROUP], U16, name="offs_sb")
+        near_sb = keep.tile([P, S // GROUP], U16, name="near_sb")
+        far_sb = keep.tile([P, S // GROUP], U16, name="far_sb")
         xw = tile("xw", [P, T], I32)
         xs = tile("xs", [P, T], U8)
         xw_pick = tile("xw_pick", [P, S], U32)
         xs_pick = tile("xs_pick", [P, S], U8)
-        warm = keep.tile([P, 2], F32, name="warm")
 
-        w_raw = tiles("w_raw", [P, PACK, H], F32, 3)
+        w1_raw = tile("w1_raw", [P, PACK, H], F32)
+        w2_raw = tiles("w2_raw", [P, PACK, HALF], F32, 2)
+        w3_raw = tile("w3_raw", [P, PACK, N], F32)
         w_codes = tiles("w_codes", [P, H], U32, 3)
         w_scales = tiles("w_scales", [P, H], U8, 3)
 
-        ba_sb = tiles("ba", [P, 2 * S], F32, PACK)
-        b_sb = [ba_sb[t][:, 0:S] for t in range(PACK)]
-        a_sb = [ba_sb[t ^ 1][:, S : 2 * S] for t in range(PACK)]
-        an_sb = tiles("an", [P, S], F32, PACK)
-        g1_sb = tiles("g1", [P, S], F32, PACK)
-        b2_sb = tiles("b2", [P, S], F32, PACK)
+        b_window = tiles("b_window", [P, 2 * S], F32, PACK)
+        b_sb = [b_window[t][:, 0:S] for t in range(PACK)]
+        a_sb = [b_window[t ^ 1][:, S : 2 * S] for t in range(PACK)]
+        a_near = tiles("a_near", [P, S], F32, PACK)
+        step_tmp = tiles("step_tmp", [P, S], F32, PACK)
+        b2_window = tiles("b2_window", [P, S], F32, PACK)
         b2_all = tile("b2_all", [P, PACK, S], F32)
-        g2_all = tile("g2_all", [P, PACK, 384], F32)
+        far_term = tile("far_term", [P, PACK, TAIL], F32)
         z_bf = tile("z_bf", [P, PACK * S], BF16)
         z_codes = tile("z_codes", [P, S], U32)
         z_scales = tile("z_scales", [P, S], U8)
 
-        def load_weight(i, w):
-            nc.sync.dma_start(out=w_raw[i][:], in_=w.rearrange("(p j) c -> p j c", j=PACK))
+        def load_weight(raw, w):
+            nc.sync.dma_start(out=raw[:], in_=w.rearrange("(p j) c -> p j c", j=PACK))
 
         nc.gpsimd.memset(xs[:].bitcast(I32), 0)
-        nc.sync.dma_start(offs_sb[:], offs)
         nc.sync.dma_start(out=xw[:], in_=x_words[0].rearrange("p n t -> p (n t)").bitcast(I32))
+        nc.sync.dma_start(offs_sb[:], offs)
         for q in range(4):
             nc.sync.dma_start(
                 out=xs[32 * q : 32 * q + 4, :].bitcast(I32), in_=x_scales[0, 4 * q : 4 * q + 4, :].bitcast(I32)
             )
-        load_weight(0, w1)
-        nc.gpsimd.memset(warm[:, 0:1], 0.0)
-        nc.scalar.activation(warm[:, 1:2], warm[:, 0:1], SIGMOID)
+        load_weight(w1_raw, w1)
+        load_weight(w2_raw[0], w2[:, 0:HALF])
+        load_weight(w2_raw[1], w2[:, HALF:H])
         nc.sync.dma_start(near_sb[:], near)
-        load_weight(1, w2)
         nc.sync.dma_start(far_sb[:], far)
-        load_weight(2, w3)
+        load_weight(w3_raw, w3)
 
-        def cast_dealt(copy, i, t0, tag):
-            values = tile(tag, [P, 2 * H], BF16)
-            dst = values[:].rearrange("p (t m j) -> p m j t", t=2, j=PACK)
-            src = w_raw[i][:].rearrange("p j (m t) -> p m j t", t=PACK)
-            copy(dst, src[:, :, :, t0 : t0 + 2])
-            return values
+        nc.vector.tensor_copy(xw_pick[:], xw[:].bitcast(U32).indirect(offs_sb[:]))
+        nc.vector.tensor_copy(xs_pick[:], xs[:].indirect(offs_sb[:]))
+
+        def cast_dealt(pair, raw, t0, m0):
+            dst = pair[:].rearrange("p (t m j) -> p m j t", t=2, j=PACK)
+            src = raw[:].rearrange("p j (m t) -> p m j t", t=PACK)
+            nc.vector.tensor_copy(dst[:, m0 : m0 + src.shape[1]], src[:, :, :, t0 : t0 + 2])
 
         def quantize(codes, scales, c0, c1, values):
             nc.vector.quantize_mx(out=codes[:, c0:c1].bitcast(FP8X4), scales=scales[:, c0:c1], in_=values)
 
-        def first_product(i, t, name):
-            acc = psum.tile([P, S], F32, name=name)
-            cols = slice(P * t, P * (t + 1))
+        def product(acc, i, tile_no, codes, scales):
+            cols = slice(P * tile_no, P * (tile_no + 1))
             nc.tensor.matmul_mx(
-                out=acc[:],
+                out=acc,
                 lhsT=w_codes[i][:, cols].bitcast(FP8X4),
                 lhsT_scale=w_scales[i][:, cols],
-                rhs=xw_pick[:].bitcast(FP8X4),
-                rhs_scale=xs_pick[:],
+                rhs=codes.bitcast(FP8X4),
+                rhs_scale=scales,
                 start=True,
                 stop=True,
             )
+
+        def first_product(i, t, bank, c0=0, c1=S):
+            acc = psum.tile([P, c1 - c0], F32, name="bank%d" % bank)
+            product(acc[:], i, t, xw_pick[:, c0:c1], xs_pick[:, c0:c1])
             return acc
 
-        nc.vector.tensor_copy(xw_pick[:], xw[:].bitcast(U32).indirect(offs_sb[:]))
-        nc.vector.tensor_copy(xs_pick[:], xs[:].indirect(offs_sb[:]))
-        w1_low = cast_dealt(nc.vector.tensor_copy, 0, 0, "w1_low")
-        w1_high = cast_dealt(nc.scalar.copy, 0, 2, "w1_high")
+        w1_low, w1_high, w2_low, w2_high = tiles("w_pair", [P, 2 * H], BF16, 4)
+        cast_dealt(w1_low, w1_raw, 0, 0)
         quantize(w_codes[0], w_scales[0], 0, 2 * P, w1_low[:])
+        cast_dealt(w1_high, w1_raw, 2, 0)
         quantize(w_codes[0], w_scales[0], 2 * P, 4 * P, w1_high[:])
-        u_ps = [first_product(0, t, "bank%d" % t) for t in range(PACK - 1)]
-        w2_low = cast_dealt(nc.vector.tensor_copy, 1, 0, "w2_pair")
+        u_ps = [first_product(0, t, t) for t in range(PACK - 1)]
+
+        cast_dealt(w2_low, w2_raw[0], 0, 0)
+        cast_dealt(w2_high, w2_raw[0], 2, 0)
+        cast_dealt(w2_low, w2_raw[1], 0, HALF // PACK)
         quantize(w_codes[1], w_scales[1], 0, P, w2_low[:, 0:H])
         quantize(w_codes[1], w_scales[1], P, 2 * P, w2_low[:, H : 2 * H])
-        w2_high = cast_dealt(nc.vector.tensor_copy, 1, 2, "w2_pair")
+        cast_dealt(w2_high, w2_raw[1], 2, HALF // PACK)
         quantize(w_codes[1], w_scales[1], 2 * P, 4 * P, w2_high[:])
-        b_ps = [first_product(1, t, "bank%d" % (PACK - 1 + t)) for t in range(2)]
-        a2_sb = g1_sb
+        b0_ps = [first_product(1, 0, 3 + h, HALF * h, HALF * (h + 1)) for h in range(2)]
+        b1_ps = first_product(1, 1, 5)
 
         def decay(t):
             nc.scalar.activation(a_sb[t], u_ps[t][:], SIGMOID)
 
-        def decay_near(t, tag):
-            u_sb = tile(tag, [P, S], F32)
-            nc.scalar.copy(u_sb[:], u_ps[t][:])
-            for h in range(2):
-                lst = near_sb[:, 16 * h : 16 * (h + 1)]
-                nc.scalar.activation(an_sb[t][:, HALF * h : HALF * (h + 1)], u_sb[:].indirect(lst), SIGMOID)
-
-        def carry_in(t):
-            nc.scalar.copy(b_sb[t], b_ps[t][:])
-
-        def carry_near(t):
-            nc.vector.tensor_tensor(g1_sb[t][:], ba_sb[t][:].indirect(near_sb[:]), a_sb[t], MULT)
-
-        def first_step(t):
-            nc.vector.tensor_tensor(b2_sb[t][:], g1_sb[t][:], b_sb[t], ADD)
-
-        def decay_product(t):
-            nc.vector.tensor_tensor(a2_sb[t][:], a_sb[t], an_sb[t][:], MULT)
-
         for t in range(PACK - 1):
             decay(t)
-        carry_in(0)
-        u_ps.append(first_product(0, 3, "bank3"))
-        b_ps.extend(first_product(1, t, "bank%d" % (PACK - 1 + t)) for t in range(2, PACK))
-        carry_in(1)
+        for h in range(2):
+            nc.scalar.copy(b_sb[0][:, HALF * h : HALF * (h + 1)], b0_ps[h][:])
+        u_ps.append(first_product(0, 3, 3))
+        b2_ps, b3_ps = first_product(1, 2, 6), first_product(1, 3, 7)
+        nc.scalar.copy(b_sb[1], b1_ps[:])
         decay(3)
-        carry_in(2)
-        carry_in(3)
+        nc.scalar.copy(b_sb[2], b2_ps[:])
+        nc.scalar.copy(b_sb[3], b3_ps[:])
+
+        u_slots = ("w_codes1", "w_scales1")
         for t in range(PACK):
-            decay_near(t, "w_codes1" if t % 2 == 0 else "w_scales1")
-        carry_near(0)
-        carry_near(1)
-        first_step(0)
-        carry_near(2)
-        first_step(1)
+            u_window = tile(u_slots[t % 2], [P, S], F32)
+            nc.scalar.copy(u_window[:], u_ps[t][:])
+            for h in range(2):
+                lst = near_sb[:, HALF // GROUP * h : HALF // GROUP * (h + 1)]
+                nc.scalar.activation(a_near[t][:, HALF * h : HALF * (h + 1)], u_window[:].indirect(lst), SIGMOID)
+
+        def near_term(t):
+            nc.vector.tensor_tensor(step_tmp[t][:], b_window[t][:].indirect(near_sb[:]), a_sb[t], MULT)
+
+        def near_sum(t):
+            nc.vector.tensor_tensor(b2_window[t][:], step_tmp[t][:], b_sb[t], ADD)
+
+        def decay_product(t):
+            nc.vector.tensor_tensor(step_tmp[t][:], a_sb[t], a_near[t][:], MULT)
+
+        near_term(0)
+        near_term(1)
+        near_sum(0)
+        near_term(2)
+        near_sum(1)
         decay_product(0)
-        carry_near(3)
-        first_step(2)
+        near_term(3)
+        near_sum(2)
         decay_product(1)
-        first_step(3)
-        decay_product(2)
-        decay_product(3)
+        near_sum(3)
+
         for t in range(PACK):
-            nc.scalar.copy(b2_all[:, t, :], b2_sb[t][:])
-        w3_bf = tile("w_scales1", [P, PACK * N], BF16)
+            nc.scalar.copy(b2_all[:, t, :], b2_window[t][:])
+        w3_bf = tile(u_slots[1], [P, PACK * N], BF16)
         nc.scalar.copy(
-            w3_bf[:].rearrange("p (c i j) -> p c j i", i=2, j=PACK), w_raw[2][:].rearrange("p j (c i) -> p c j i", i=2)
+            w3_bf[:].rearrange("p (c i j) -> p c j i", i=2, j=PACK), w3_raw[:].rearrange("p j (c i) -> p c j i", i=2)
         )
 
-        out_rows = out.rearrange("(r p) s -> p r s", p=P)
+        def far_gather(t, c0, c1):
+            lst = far_sb[:, c0 // GROUP : c1 // GROUP]
+            nc.vector.tensor_tensor(far_term[:, t, 0 : c1 - c0], b2_window[t][:].indirect(lst), step_tmp[t][:, c0:c1], MULT)
 
-        def carry_far(c0, c1, g0):
-            for t in range(PACK):
-                nc.vector.tensor_tensor(
-                    g2_all[:, t, g0 : g0 + c1 - c0], b2_sb[t][:].indirect(far_sb[:, c0 // 16 : c1 // 16]), a2_sb[t][:, c0:c1], MULT
-                )
-
-        def second_step(c0, c1, g0):
+        def far_sum(c0, c1, f0):
             nc.vector.tensor_tensor(
                 z_bf[:, PACK * c0 : PACK * c1].rearrange("p (c i t) -> p c t i", i=2, t=PACK),
-                g2_all[:, :, g0 : g0 + c1 - c0].rearrange("p t (c i) -> p c t i", i=2),
+                far_term[:, :, f0 : f0 + c1 - c0].rearrange("p t (c i) -> p c t i", i=2),
                 b2_all[:, :, c0:c1].rearrange("p t (c i) -> p c t i", i=2),
                 ADD,
             )
+
+        out_rows = out.rearrange("(r p) s -> p r s", p=P)
 
         def last_product(n):
             c0, c1 = OUT_CHUNKS[n]
@@ -194,30 +196,25 @@ def tile_picked_scan2_none_p_kernel(
             for pair in range(2):
                 acc = psum.tile([P, 2, c1 - c0], F32, name="bank%d" % ((4 + 2 * n + pair) % 8))
                 for r in range(2):
-                    cols = slice(P * (2 * pair + r), P * (2 * pair + r + 1))
-                    nc.tensor.matmul_mx(
-                        out=acc[:, r, :],
-                        lhsT=w_codes[2][:, cols].bitcast(FP8X4),
-                        lhsT_scale=w_scales[2][:, cols],
-                        rhs=z_codes[:, c0:c1].bitcast(FP8X4),
-                        rhs_scale=z_scales[:, c0:c1],
-                        start=True,
-                        stop=True,
-                    )
+                    product(acc[:, r, :], 2, 2 * pair + r, z_codes[:, c0:c1], z_scales[:, c0:c1])
                 rows = slice(2 * pair, 2 * pair + 2)
-                if pair == 1 and c1 == S:
-                    nc.vector.tensor_copy(res[:, rows, :], acc[:])
-                else:
-                    nc.scalar.copy(res[:, rows, :], acc[:])
-                queue = nc.scalar if pair == 0 and c1 == S else nc.sync
+                copy = nc.vector.tensor_copy if c1 == S and pair == 1 else nc.scalar.copy
+                queue = nc.scalar if c1 == S and pair == 0 else nc.sync
+                copy(res[:, rows, :], acc[:])
                 queue.dma_start(out=out_rows[:, rows, c0:c1], in_=res[:, rows, :])
 
-        carry_far(0, 384, 0)
-        second_step(0, 256, 0)
-        second_step(256, 384, 256)
+        far_gather(0, 0, TAIL)
+        decay_product(2)
+        far_gather(1, 0, TAIL)
+        decay_product(3)
+        far_gather(2, 0, TAIL)
+        far_gather(3, 0, TAIL)
+        far_sum(0, HALF, 0)
+        far_sum(HALF, TAIL, HALF)
         quantize(w_codes[2], w_scales[2], 0, N, w3_bf[:])
         last_product(0)
-        carry_far(384, 512, 0)
+        for t in range(PACK):
+            far_gather(t, TAIL, S)
         last_product(1)
-        second_step(384, 512, 0)
+        far_sum(TAIL, S, 0)
         last_product(2)

@@ -15,13 +15,13 @@ FP8X4 = mybir.dt.float8_e4m3fn_x4
 MULT = mybir.AluOpType.mult
 ADD = mybir.AluOpType.add
 SIGMOID = mybir.ActivationFunctionType.Sigmoid
+COPY = mybir.ActivationFunctionType.Copy
 
 P = 128
 PACK = 4
 GROUP = 16
 HALF = 256
-TAIL = S - P
-OUT_CHUNKS = ((0, HALF), (HALF, TAIL), (TAIL, S))
+CHUNKS = ((0, HALF), (HALF, HALF + P), (HALF + P, S))
 
 
 def tile_picked_scan2_none_p_kernel(
@@ -52,14 +52,13 @@ def tile_picked_scan2_none_p_kernel(
         w_codes = tiles("w_codes", [P, H], U32, 3)
         w_scales = tiles("w_scales", [P, H], U8, 3)
 
+        a_window = tiles("a_window", [P, 2 * S], F32, PACK)
         b_window = tiles("b_window", [P, 2 * S], F32, PACK)
-        b_sb = [b_window[t][:, 0:S] for t in range(PACK)]
-        a_sb = [b_window[t ^ 1][:, S : 2 * S] for t in range(PACK)]
-        a_near = tiles("a_near", [P, S], F32, PACK)
-        step_tmp = tiles("step_tmp", [P, S], F32, PACK)
-        b2_window = tiles("b2_window", [P, S], F32, PACK)
+        a_sb = [w[:, 0:S] for w in a_window]
+        b_sb = [w[:, 0:S] for w in b_window]
+        b2_sb = tiles("b2_sb", [P, S], F32, PACK)
+        near_term = tiles("near_term", [P, S], F32, PACK)
         b2_all = tile("b2_all", [P, PACK, S], F32)
-        far_term = tile("far_term", [P, PACK, TAIL], F32)
         z_bf = tile("z_bf", [P, PACK * S], BF16)
         z_codes = tile("z_codes", [P, S], U32)
         z_scales = tile("z_scales", [P, S], U8)
@@ -67,22 +66,21 @@ def tile_picked_scan2_none_p_kernel(
         def load_weight(raw, w):
             nc.sync.dma_start(out=raw[:], in_=w.rearrange("(p j) c -> p j c", j=PACK))
 
-        nc.gpsimd.memset(xs[:].bitcast(I32), 0)
-        nc.sync.dma_start(out=xw[:], in_=x_words[0].rearrange("p n t -> p (n t)").bitcast(I32))
+        nc.vector.memset(xs[:].bitcast(I32), 0)
+        load_weight(w1_raw, w1)
+        for w in a_window + b_window:
+            nc.gpsimd.memset(w[:, S : 2 * S], 0.0)
         nc.sync.dma_start(offs_sb[:], offs)
         for q in range(4):
             nc.sync.dma_start(
                 out=xs[32 * q : 32 * q + 4, :].bitcast(I32), in_=x_scales[0, 4 * q : 4 * q + 4, :].bitcast(I32)
             )
-        load_weight(w1_raw, w1)
+        nc.sync.dma_start(out=xw[:], in_=x_words[0].rearrange("p n t -> p (n t)").bitcast(I32))
         load_weight(w2_raw[0], w2[:, 0:HALF])
         load_weight(w2_raw[1], w2[:, HALF:H])
         nc.sync.dma_start(near_sb[:], near)
         nc.sync.dma_start(far_sb[:], far)
         load_weight(w3_raw, w3)
-
-        nc.vector.tensor_copy(xw_pick[:], xw[:].bitcast(U32).indirect(offs_sb[:]))
-        nc.vector.tensor_copy(xs_pick[:], xs[:].indirect(offs_sb[:]))
 
         def cast_dealt(pair, raw, t0, m0):
             dst = pair[:].rearrange("p (t m j) -> p m j t", t=2, j=PACK)
@@ -104,85 +102,93 @@ def tile_picked_scan2_none_p_kernel(
                 stop=True,
             )
 
-        def first_product(i, t, bank, c0=0, c1=S):
-            acc = psum.tile([P, c1 - c0], F32, name="bank%d" % bank)
-            product(acc[:], i, t, xw_pick[:, c0:c1], xs_pick[:, c0:c1])
+        def first_product(i, t, bank):
+            acc = psum.tile([P, S], F32, name="bank%d" % bank)
+            product(acc[:], i, t, xw_pick[:], xs_pick[:])
             return acc
+
+        def offsets(lst, c0, c1):
+            return lst[:, c0 // GROUP : c1 // GROUP]
 
         w1_low, w1_high, w2_low, w2_high = tiles("w_pair", [P, 2 * H], BF16, 4)
         cast_dealt(w1_low, w1_raw, 0, 0)
-        quantize(w_codes[0], w_scales[0], 0, 2 * P, w1_low[:])
         cast_dealt(w1_high, w1_raw, 2, 0)
+        quantize(w_codes[0], w_scales[0], 0, 2 * P, w1_low[:])
+        nc.vector.tensor_copy(xs_pick[:], xs[:].indirect(offs_sb[:]))
         quantize(w_codes[0], w_scales[0], 2 * P, 4 * P, w1_high[:])
-        u_ps = [first_product(0, t, t) for t in range(PACK - 1)]
+        for h in range(2):
+            cols = slice(HALF * h, HALF * (h + 1))
+            nc.vector.tensor_copy(xw_pick[:, cols], xw[:].bitcast(U32).indirect(offsets(offs_sb, cols.start, cols.stop)))
+            for pair in range(2):
+                acc = psum.tile([P, 2, HALF], F32, name="bank%d" % (2 * h + pair))
+                for r in range(2):
+                    product(acc[:, r, :], 0, 2 * pair + r, xw_pick[:, cols], xs_pick[:, cols])
+                for r in range(2):
+                    nc.scalar.activation(a_sb[2 * pair + r][:, cols], acc[:, r, :], SIGMOID)
 
         cast_dealt(w2_low, w2_raw[0], 0, 0)
         cast_dealt(w2_high, w2_raw[0], 2, 0)
         cast_dealt(w2_low, w2_raw[1], 0, HALF // PACK)
+        cast_dealt(w2_high, w2_raw[1], 2, HALF // PACK)
         quantize(w_codes[1], w_scales[1], 0, P, w2_low[:, 0:H])
         quantize(w_codes[1], w_scales[1], P, 2 * P, w2_low[:, H : 2 * H])
-        cast_dealt(w2_high, w2_raw[1], 2, HALF // PACK)
         quantize(w_codes[1], w_scales[1], 2 * P, 4 * P, w2_high[:])
-        b0_ps = [first_product(1, 0, 3 + h, HALF * h, HALF * (h + 1)) for h in range(2)]
-        b1_ps = first_product(1, 1, 5)
-
-        def decay(t):
-            nc.scalar.activation(a_sb[t], u_ps[t][:], SIGMOID)
-
-        for t in range(PACK - 1):
-            decay(t)
-        for h in range(2):
-            nc.scalar.copy(b_sb[0][:, HALF * h : HALF * (h + 1)], b0_ps[h][:])
-        u_ps.append(first_product(0, 3, 3))
-        b2_ps, b3_ps = first_product(1, 2, 6), first_product(1, 3, 7)
-        nc.scalar.copy(b_sb[1], b1_ps[:])
-        decay(3)
-        nc.scalar.copy(b_sb[2], b2_ps[:])
-        nc.scalar.copy(b_sb[3], b3_ps[:])
-
-        u_slots = ("w_codes1", "w_scales1")
+        b_ps = [first_product(1, t, PACK + t) for t in range(PACK)]
         for t in range(PACK):
-            u_window = tile(u_slots[t % 2], [P, S], F32)
-            nc.scalar.copy(u_window[:], u_ps[t][:])
-            for h in range(2):
-                lst = near_sb[:, HALF // GROUP * h : HALF // GROUP * (h + 1)]
-                nc.scalar.activation(a_near[t][:, HALF * h : HALF * (h + 1)], u_window[:].indirect(lst), SIGMOID)
+            nc.scalar.copy(b_sb[t], b_ps[t][:])
 
-        def near_term(t):
-            nc.vector.tensor_tensor(step_tmp[t][:], b_window[t][:].indirect(near_sb[:]), a_sb[t], MULT)
+        a_near = tile("w_codes1", [P, PACK - 1, S], F32)
+        b_near = tile("w_scales1", [P, S], F32)
+        nc.scalar.activation(a_near[:, 0, :], a_window[1][:].indirect(near_sb[:]), COPY)
+        nc.scalar.activation(b_near[:], b_window[PACK - 1][:].indirect(near_sb[:]), COPY)
+        for t in range(2, PACK):
+            nc.scalar.activation(a_near[:, t - 1, :], a_window[t][:].indirect(near_sb[:]), COPY)
+
+        def near_gather(t):
+            if t == PACK - 1:
+                nc.vector.tensor_tensor(near_term[t][:], b_near[:], a_sb[t], MULT)
+            else:
+                nc.vector.tensor_tensor(near_term[t][:], b_window[t][:].indirect(near_sb[:]), a_sb[t], MULT)
+
+        a_near_first = tile("w_pair3", [P, S], F32)
+        nc.vector.tensor_copy(a_near_first[:], a_window[0][:].indirect(near_sb[:]))
+        a2_all = tile("a2_all", [P, PACK, S], F32)
 
         def near_sum(t):
-            nc.vector.tensor_tensor(b2_window[t][:], step_tmp[t][:], b_sb[t], ADD)
+            nc.vector.tensor_tensor(b2_sb[t][:], near_term[t][:], b_sb[t], ADD)
+            nc.sync.dma_start(out=b2_all[:, t, :], in_=b2_sb[t][:])
 
         def decay_product(t):
-            nc.vector.tensor_tensor(step_tmp[t][:], a_sb[t], a_near[t][:], MULT)
+            nc.vector.tensor_tensor(a2_all[:, t, :], a_sb[t], a_near[:, t - 1, :] if t else a_near_first[:], MULT)
 
-        near_term(0)
-        near_term(1)
-        near_sum(0)
-        near_term(2)
-        near_sum(1)
+        near_gather(0)
+        for t in range(1, PACK):
+            near_gather(t)
+            near_sum(t - 1)
         decay_product(0)
-        near_term(3)
-        near_sum(2)
-        decay_product(1)
-        near_sum(3)
+        near_sum(PACK - 1)
+        for t in range(1, PACK):
+            decay_product(t)
 
-        for t in range(PACK):
-            nc.scalar.copy(b2_all[:, t, :], b2_window[t][:])
-        w3_bf = tile(u_slots[1], [P, PACK * N], BF16)
-        nc.scalar.copy(
-            w3_bf[:].rearrange("p (c i j) -> p c j i", i=2, j=PACK), w3_raw[:].rearrange("p j (c i) -> p c j i", i=2)
-        )
+        b2_far_head = tile("b2_far_head", [P, PACK, HALF], F32)
+        b2_far_tail = tile("near_term3", [P, PACK, HALF], F32)
+        b2_far = [b2_far_head[:], b2_far_tail[:, :, 0:P], b2_far_tail[:, :, P:HALF]]
+        far_term = [tile("far_term", [P, PACK, HALF], F32)[:]]
 
-        def far_gather(t, c0, c1):
-            lst = far_sb[:, c0 // GROUP : c1 // GROUP]
-            nc.vector.tensor_tensor(far_term[:, t, 0 : c1 - c0], b2_window[t][:].indirect(lst), step_tmp[t][:, c0:c1], MULT)
+        def far_gather(n):
+            c0, c1 = CHUNKS[n]
+            for t in range(PACK):
+                nc.scalar.activation(b2_far[n][:, t, :], b2_sb[t][:].indirect(offsets(far_sb, c0, c1)), COPY)
 
-        def far_sum(c0, c1, f0):
+        def far_product(n):
+            c0, c1 = CHUNKS[n]
+            nc.vector.tensor_tensor(far_term[n], b2_far[n], a2_all[:, :, c0:c1], MULT)
+
+        def far_sum(n):
+            c0, c1 = CHUNKS[n]
             nc.vector.tensor_tensor(
                 z_bf[:, PACK * c0 : PACK * c1].rearrange("p (c i t) -> p c t i", i=2, t=PACK),
-                far_term[:, :, f0 : f0 + c1 - c0].rearrange("p t (c i) -> p c t i", i=2),
+                far_term[n].rearrange("p t (c i) -> p c t i", i=2),
                 b2_all[:, :, c0:c1].rearrange("p t (c i) -> p c t i", i=2),
                 ADD,
             )
@@ -190,11 +196,11 @@ def tile_picked_scan2_none_p_kernel(
         out_rows = out.rearrange("(r p) s -> p r s", p=P)
 
         def last_product(n):
-            c0, c1 = OUT_CHUNKS[n]
+            c0, c1 = CHUNKS[n]
             quantize(z_codes, z_scales, c0, c1, z_bf[:, PACK * c0 : PACK * c1])
             res = keep.tile([P, PACK, c1 - c0], F32, name="res%d" % n)
             for pair in range(2):
-                acc = psum.tile([P, 2, c1 - c0], F32, name="bank%d" % ((4 + 2 * n + pair) % 8))
+                acc = psum.tile([P, 2, c1 - c0], F32, name="bank%d" % (2 * n + pair))
                 for r in range(2):
                     product(acc[:, r, :], 2, 2 * pair + r, z_codes[:, c0:c1], z_scales[:, c0:c1])
                 rows = slice(2 * pair, 2 * pair + 2)
@@ -203,18 +209,29 @@ def tile_picked_scan2_none_p_kernel(
                 copy(res[:, rows, :], acc[:])
                 queue.dma_start(out=out_rows[:, rows, c0:c1], in_=res[:, rows, :])
 
-        far_gather(0, 0, TAIL)
-        decay_product(2)
-        far_gather(1, 0, TAIL)
-        decay_product(3)
-        far_gather(2, 0, TAIL)
-        far_gather(3, 0, TAIL)
-        far_sum(0, HALF, 0)
-        far_sum(HALF, TAIL, HALF)
-        quantize(w_codes[2], w_scales[2], 0, N, w3_bf[:])
+        def cast_w3(h, slot, copy):
+            values = tile(slot, [P, PACK * HALF], BF16)
+            copy(
+                values[:].rearrange("p (c i j) -> p c j i", i=2, j=PACK),
+                w3_raw[:, :, HALF * h : HALF * (h + 1)].rearrange("p j (c i) -> p c j i", i=2),
+            )
+            return values
+
+        far_gather(0)
+        w3_low = cast_w3(0, "near_term2", nc.vector.tensor_copy)
+        w3_high = cast_w3(1, "b_window3", nc.scalar.copy)
+        far_gather(1)
+        far_gather(2)
+        far_product(0)
+        quantize(w_codes[2], w_scales[2], 0, HALF, w3_low[:])
+        far_sum(0)
+        quantize(w_codes[2], w_scales[2], HALF, N, w3_high[:])
+        far_term_tail = tile("far_term", [P, PACK, HALF], F32)
+        far_term.extend([far_term_tail[:, :, 0:P], far_term_tail[:, :, P:HALF]])
+        far_product(1)
         last_product(0)
-        for t in range(PACK):
-            far_gather(t, TAIL, S)
+        far_sum(1)
+        far_product(2)
         last_product(1)
-        far_sum(TAIL, S, 0)
+        far_sum(2)
         last_product(2)

@@ -69,7 +69,7 @@ def tile_picked_scan2_none_p_kernel(
         nc.vector.memset(xs[:].bitcast(I32), 0)
         load_weight(w1_raw, w1)
         for w in a_window + b_window:
-            nc.gpsimd.memset(w[:, S : 2 * S], 0.0)
+            nc.vector.memset(w[:, S : 2 * S], 0.0)
         nc.sync.dma_start(offs_sb[:], offs)
         for q in range(4):
             nc.sync.dma_start(
@@ -156,7 +156,8 @@ def tile_picked_scan2_none_p_kernel(
 
         def near_sum(t):
             nc.vector.tensor_tensor(b2_sb[t][:], near_term[t][:], b_sb[t], ADD)
-            nc.sync.dma_start(out=b2_all[:, t, :], in_=b2_sb[t][:])
+            if t < PACK - 1:
+                nc.sync.dma_start(out=b2_all[:, t, :], in_=b2_sb[t][:])
 
         def decay_product(t):
             nc.vector.tensor_tensor(a2_all[:, t, :], a_sb[t], a_near[:, t - 1, :] if t else a_near_first[:], MULT)
@@ -169,6 +170,7 @@ def tile_picked_scan2_none_p_kernel(
         near_sum(PACK - 1)
         for t in range(1, PACK):
             decay_product(t)
+        nc.vector.tensor_copy(b2_all[:, PACK - 1, :], b2_sb[PACK - 1][:])
 
         b2_far_head = tile("b2_far_head", [P, PACK, HALF], F32)
         b2_far_tail = tile("near_term3", [P, PACK, HALF], F32)

@@ -57,7 +57,10 @@ def tile_picked_scan2_none_p_kernel(
         a_sb = [w[:, 0:S] for w in a_window]
         b_sb = [w[:, 0:S] for w in b_window]
         b2_sb = tiles("b2_sb", [P, S], F32, PACK)
-        near_term = tiles("near_term", [P, S], F32, PACK)
+        spare = lambda window: window[:, S : 2 * S]
+        near_term = [spare(a_window[1]), spare(b_window[2])] + [tile("near_term%d" % t, [P, S], F32)[:] for t in (2, 3)]
+        a_near = [spare(b_window[1]), spare(a_window[3])] + [tile("a_near%d" % t, [P, S], F32)[:] for t in (2, 3)]
+        b_near = spare(a_window[2])
         b2_all = tile("b2_all", [P, PACK, S], F32)
         z_bf = tile("z_bf", [P, PACK * S], BF16)
         z_codes = tile("z_codes", [P, S], U32)
@@ -68,13 +71,11 @@ def tile_picked_scan2_none_p_kernel(
 
         nc.vector.memset(xs[:].bitcast(I32), 0)
         load_weight(w1_raw, w1)
-        for w in a_window + b_window:
-            nc.vector.memset(w[:, S : 2 * S], 0.0)
+        for w in (a_window[0], b_window[0], b_window[3]):
+            nc.vector.memset(spare(w), 0.0)
         nc.sync.dma_start(offs_sb[:], offs)
-        for q in range(4):
-            nc.sync.dma_start(
-                out=xs[32 * q : 32 * q + 4, :].bitcast(I32), in_=x_scales[0, 4 * q : 4 * q + 4, :].bitcast(I32)
-            )
+        for r in range(4):
+            nc.sync.dma_start(out=xs[r:P:32, :].bitcast(I32), in_=x_scales[0, r:16:4, :].bitcast(I32))
         nc.sync.dma_start(out=xw[:], in_=x_words[0].rearrange("p n t -> p (n t)").bitcast(I32))
         load_weight(w2_raw[0], w2[:, 0:HALF])
         load_weight(w2_raw[1], w2[:, HALF:H])
@@ -116,15 +117,17 @@ def tile_picked_scan2_none_p_kernel(
         quantize(w_codes[0], w_scales[0], 0, 2 * P, w1_low[:])
         nc.vector.tensor_copy(xs_pick[:], xs[:].indirect(offs_sb[:]))
         quantize(w_codes[0], w_scales[0], 2 * P, 4 * P, w1_high[:])
-        for h in range(2):
-            cols = slice(HALF * h, HALF * (h + 1))
-            nc.vector.tensor_copy(xw_pick[:, cols], xw[:].bitcast(U32).indirect(offsets(offs_sb, cols.start, cols.stop)))
-            for pair in range(2):
-                acc = psum.tile([P, 2, HALF], F32, name="bank%d" % (2 * h + pair))
-                for r in range(2):
-                    product(acc[:, r, :], 0, 2 * pair + r, xw_pick[:, cols], xs_pick[:, cols])
-                for r in range(2):
-                    nc.scalar.activation(a_sb[2 * pair + r][:, cols], acc[:, r, :], SIGMOID)
+        bank = 0
+        for c0, groups in ((0, ((0,), (1,), (2, 3))), (HALF, ((0, 1), (2, 3)))):
+            cols = slice(c0, c0 + HALF)
+            nc.vector.tensor_copy(xw_pick[:, cols], xw[:].bitcast(U32).indirect(offsets(offs_sb, c0, c0 + HALF)))
+            for group in groups:
+                acc = psum.tile([P, len(group), HALF], F32, name="bank%d" % bank)
+                bank += 1
+                for r, t in enumerate(group):
+                    product(acc[:, r, :], 0, t, xw_pick[:, cols], xs_pick[:, cols])
+                for r, t in enumerate(group):
+                    nc.scalar.activation(a_sb[t][:, cols], acc[:, r, :], SIGMOID)
 
         cast_dealt(w2_low, w2_raw[0], 0, 0)
         cast_dealt(w2_high, w2_raw[0], 2, 0)
@@ -133,35 +136,39 @@ def tile_picked_scan2_none_p_kernel(
         quantize(w_codes[1], w_scales[1], 0, P, w2_low[:, 0:H])
         quantize(w_codes[1], w_scales[1], P, 2 * P, w2_low[:, H : 2 * H])
         quantize(w_codes[1], w_scales[1], 2 * P, 4 * P, w2_high[:])
-        b_ps = [first_product(1, t, PACK + t) for t in range(PACK)]
+        b_ps = [first_product(1, t, (5 + t) % 8) for t in range(PACK)]
+        nc.vector.tensor_copy(a_near[0], a_window[0][:].indirect(near_sb[:]))
         for t in range(PACK):
             nc.scalar.copy(b_sb[t], b_ps[t][:])
 
-        a_near = tile("w_codes1", [P, PACK - 1, S], F32)
-        b_near = tile("w_scales1", [P, S], F32)
-        nc.scalar.activation(a_near[:, 0, :], a_window[1][:].indirect(near_sb[:]), COPY)
-        nc.scalar.activation(b_near[:], b_window[PACK - 1][:].indirect(near_sb[:]), COPY)
-        for t in range(2, PACK):
-            nc.scalar.activation(a_near[:, t - 1, :], a_window[t][:].indirect(near_sb[:]), COPY)
+        nc.scalar.activation(b_near, b_window[PACK - 1][:].indirect(near_sb[:]), COPY)
+        for t in range(1, PACK):
+            nc.scalar.activation(a_near[t], a_window[t][:].indirect(near_sb[:]), COPY)
+
+        def cast_w3(h, slot, copy):
+            values = tile(slot, [P, PACK * HALF], BF16)
+            copy(
+                values[:].rearrange("p (c i j) -> p c j i", i=2, j=PACK),
+                w3_raw[:, :, HALF * h : HALF * (h + 1)].rearrange("p j (c i) -> p c j i", i=2),
+            )
+            return values
 
         def near_gather(t):
             if t == PACK - 1:
-                nc.vector.tensor_tensor(near_term[t][:], b_near[:], a_sb[t], MULT)
+                nc.vector.tensor_tensor(near_term[t], b_near, a_sb[t], MULT)
             else:
-                nc.vector.tensor_tensor(near_term[t][:], b_window[t][:].indirect(near_sb[:]), a_sb[t], MULT)
+                nc.vector.tensor_tensor(near_term[t], b_window[t][:].indirect(near_sb[:]), a_sb[t], MULT)
 
-        a_near_first = tile("w_pair3", [P, S], F32)
-        nc.vector.tensor_copy(a_near_first[:], a_window[0][:].indirect(near_sb[:]))
-        a2_all = tile("a2_all", [P, PACK, S], F32)
 
         def near_sum(t):
-            nc.vector.tensor_tensor(b2_sb[t][:], near_term[t][:], b_sb[t], ADD)
-            if t < PACK - 1:
-                nc.sync.dma_start(out=b2_all[:, t, :], in_=b2_sb[t][:])
+            nc.vector.tensor_tensor(b2_sb[t][:], near_term[t], b_sb[t], ADD)
+            c0 = HALF if t == PACK - 1 else 0
+            nc.sync.dma_start(out=b2_all[:, t, c0:S], in_=b2_sb[t][:, c0:S])
 
         def decay_product(t):
-            nc.vector.tensor_tensor(a2_all[:, t, :], a_sb[t], a_near[:, t - 1, :] if t else a_near_first[:], MULT)
+            nc.vector.tensor_tensor(a2_all[:, t, :], a_sb[t], a_near[t], MULT)
 
+        a2_all = tile("a2_all", [P, PACK, S], F32)
         near_gather(0)
         for t in range(1, PACK):
             near_gather(t)
@@ -170,7 +177,7 @@ def tile_picked_scan2_none_p_kernel(
         near_sum(PACK - 1)
         for t in range(1, PACK):
             decay_product(t)
-        nc.vector.tensor_copy(b2_all[:, PACK - 1, :], b2_sb[PACK - 1][:])
+        nc.vector.tensor_copy(b2_all[:, PACK - 1, 0:HALF], b2_sb[PACK - 1][:, 0:HALF])
 
         b2_far_head = tile("b2_far_head", [P, PACK, HALF], F32)
         b2_far_tail = tile("near_term3", [P, PACK, HALF], F32)
@@ -202,7 +209,7 @@ def tile_picked_scan2_none_p_kernel(
             quantize(z_codes, z_scales, c0, c1, z_bf[:, PACK * c0 : PACK * c1])
             res = keep.tile([P, PACK, c1 - c0], F32, name="res%d" % n)
             for pair in range(2):
-                acc = psum.tile([P, 2, c1 - c0], F32, name="bank%d" % (2 * n + pair))
+                acc = psum.tile([P, 2, c1 - c0], F32, name="bank%d" % (1 + 2 * n + pair))
                 for r in range(2):
                     product(acc[:, r, :], 2, 2 * pair + r, z_codes[:, c0:c1], z_scales[:, c0:c1])
                 rows = slice(2 * pair, 2 * pair + 2)
@@ -210,14 +217,6 @@ def tile_picked_scan2_none_p_kernel(
                 queue = nc.scalar if c1 == S and pair == 0 else nc.sync
                 copy(res[:, rows, :], acc[:])
                 queue.dma_start(out=out_rows[:, rows, c0:c1], in_=res[:, rows, :])
-
-        def cast_w3(h, slot, copy):
-            values = tile(slot, [P, PACK * HALF], BF16)
-            copy(
-                values[:].rearrange("p (c i j) -> p c j i", i=2, j=PACK),
-                w3_raw[:, :, HALF * h : HALF * (h + 1)].rearrange("p j (c i) -> p c j i", i=2),
-            )
-            return values
 
         far_gather(0)
         w3_low = cast_w3(0, "near_term2", nc.vector.tensor_copy)

@@ -57,10 +57,9 @@ def tile_picked_scan2_none_p_kernel(
         a_sb = [w[:, 0:S] for w in a_window]
         b_sb = [w[:, 0:S] for w in b_window]
         b2_sb = tiles("b2_sb", [P, S], F32, PACK)
-        spare = lambda window: window[:, S : 2 * S]
-        near_term = [spare(a_window[1]), spare(b_window[2])] + [tile("near_term%d" % t, [P, S], F32)[:] for t in (2, 3)]
-        a_near = [spare(b_window[1]), spare(a_window[3])] + [tile("a_near%d" % t, [P, S], F32)[:] for t in (2, 3)]
-        b_near = spare(a_window[2])
+        near_term = [t[:] for t in tiles("near_term", [P, S], F32, PACK)]
+        a_near = [tile("a_near", [P, S], F32)[:]]
+        b_near = tile("b_near", [P, S], F32)[:]
         b2_all = tile("b2_all", [P, PACK, S], F32)
         z_bf = tile("z_bf", [P, PACK * S], BF16)
         z_codes = tile("z_codes", [P, S], U32)
@@ -71,11 +70,11 @@ def tile_picked_scan2_none_p_kernel(
 
         nc.vector.memset(xs[:].bitcast(I32), 0)
         load_weight(w1_raw, w1)
-        for w in (a_window[0], b_window[0], b_window[3]):
-            nc.vector.memset(spare(w), 0.0)
         nc.sync.dma_start(offs_sb[:], offs)
-        for r in range(4):
-            nc.sync.dma_start(out=xs[r:P:32, :].bitcast(I32), in_=x_scales[0, r:16:4, :].bitcast(I32))
+        for q in range(4):
+            nc.sync.dma_start(
+                out=xs[32 * q : 32 * q + 4, :].bitcast(I32), in_=x_scales[0, 4 * q : 4 * q + 4, :].bitcast(I32)
+            )
         nc.sync.dma_start(out=xw[:], in_=x_words[0].rearrange("p n t -> p (n t)").bitcast(I32))
         load_weight(w2_raw[0], w2[:, 0:HALF])
         load_weight(w2_raw[1], w2[:, HALF:H])
@@ -83,10 +82,10 @@ def tile_picked_scan2_none_p_kernel(
         nc.sync.dma_start(far_sb[:], far)
         load_weight(w3_raw, w3)
 
-        def cast_dealt(pair, raw, t0, m0):
-            dst = pair[:].rearrange("p (t m j) -> p m j t", t=2, j=PACK)
+        def cast_dealt(values, raw, m0, t0=0, t1=PACK):
+            dst = values[:].rearrange("p (t m j) -> p m j t", t=PACK, j=PACK)
             src = raw[:].rearrange("p j (m t) -> p m j t", t=PACK)
-            nc.vector.tensor_copy(dst[:, m0 : m0 + src.shape[1]], src[:, :, :, t0 : t0 + 2])
+            nc.vector.tensor_copy(dst[:, m0 : m0 + src.shape[1], :, t0:t1], src[:, :, :, t0:t1])
 
         def quantize(codes, scales, c0, c1, values):
             nc.vector.quantize_mx(out=codes[:, c0:c1].bitcast(FP8X4), scales=scales[:, c0:c1], in_=values)
@@ -111,47 +110,34 @@ def tile_picked_scan2_none_p_kernel(
         def offsets(lst, c0, c1):
             return lst[:, c0 // GROUP : c1 // GROUP]
 
-        w1_low, w1_high, w2_low, w2_high = tiles("w_pair", [P, 2 * H], BF16, 4)
-        cast_dealt(w1_low, w1_raw, 0, 0)
-        cast_dealt(w1_high, w1_raw, 2, 0)
-        quantize(w_codes[0], w_scales[0], 0, 2 * P, w1_low[:])
+        w1_bf, w2_bf = tiles("w_bf", [P, PACK * H], BF16, 2)
+        cast_dealt(w1_bf, w1_raw, 0, 0, 2)
+        cast_dealt(w1_bf, w1_raw, 0, 2, PACK)
+        quantize(w_codes[0], w_scales[0], 0, 2 * P, w1_bf[:, 0 : 2 * H])
+        quantize(w_codes[0], w_scales[0], 2 * P, H, w1_bf[:, 2 * H : PACK * H])
         nc.vector.tensor_copy(xs_pick[:], xs[:].indirect(offs_sb[:]))
-        quantize(w_codes[0], w_scales[0], 2 * P, 4 * P, w1_high[:])
-        bank = 0
-        for c0, groups in ((0, ((0,), (1,), (2, 3))), (HALF, ((0, 1), (2, 3)))):
-            cols = slice(c0, c0 + HALF)
-            nc.vector.tensor_copy(xw_pick[:, cols], xw[:].bitcast(U32).indirect(offsets(offs_sb, c0, c0 + HALF)))
-            for group in groups:
-                acc = psum.tile([P, len(group), HALF], F32, name="bank%d" % bank)
-                bank += 1
-                for r, t in enumerate(group):
-                    product(acc[:, r, :], 0, t, xw_pick[:, cols], xs_pick[:, cols])
-                for r, t in enumerate(group):
-                    nc.scalar.activation(a_sb[t][:, cols], acc[:, r, :], SIGMOID)
+        for c0 in (0, HALF):
+            nc.vector.tensor_copy(xw_pick[:, c0 : c0 + HALF], xw[:].bitcast(U32).indirect(offsets(offs_sb, c0, c0 + HALF)))
+        pieces = [(t, c0, c0 + HALF) for c0 in (0, HALF) for t in (0, 1)] + [(t, 0, S) for t in (2, 3)]
+        for bank, (t, c0, c1) in enumerate(pieces):
+            acc = psum.tile([P, c1 - c0], F32, name="bank%d" % bank)
+            product(acc[:], 0, t, xw_pick[:, c0:c1], xs_pick[:, c0:c1])
+            nc.scalar.activation(a_sb[t][:, c0:c1], acc[:], SIGMOID)
 
-        cast_dealt(w2_low, w2_raw[0], 0, 0)
-        cast_dealt(w2_high, w2_raw[0], 2, 0)
-        cast_dealt(w2_low, w2_raw[1], 0, HALF // PACK)
-        cast_dealt(w2_high, w2_raw[1], 2, HALF // PACK)
-        quantize(w_codes[1], w_scales[1], 0, P, w2_low[:, 0:H])
-        quantize(w_codes[1], w_scales[1], P, 2 * P, w2_low[:, H : 2 * H])
-        quantize(w_codes[1], w_scales[1], 2 * P, 4 * P, w2_high[:])
-        b_ps = [first_product(1, t, (5 + t) % 8) for t in range(PACK)]
+        cast_dealt(w2_bf, w2_raw[0], 0)
+        cast_dealt(w2_bf, w2_raw[1], HALF // PACK, 0, 2)
+        cast_dealt(w2_bf, w2_raw[1], HALF // PACK, 2, PACK)
+        quantize(w_codes[1], w_scales[1], 0, P, w2_bf[:, 0:H])
+        quantize(w_codes[1], w_scales[1], P, H, w2_bf[:, H : PACK * H])
+        b_ps = [first_product(1, t, (6 + t) % 8) for t in range(PACK)]
         nc.vector.tensor_copy(a_near[0], a_window[0][:].indirect(near_sb[:]))
         for t in range(PACK):
             nc.scalar.copy(b_sb[t], b_ps[t][:])
 
+        a_near.extend(tile(name, [P, S], F32)[:] for name in ("w_codes1", "w_scales1", "xw_pick"))
         nc.scalar.activation(b_near, b_window[PACK - 1][:].indirect(near_sb[:]), COPY)
         for t in range(1, PACK):
             nc.scalar.activation(a_near[t], a_window[t][:].indirect(near_sb[:]), COPY)
-
-        def cast_w3(h, slot, copy):
-            values = tile(slot, [P, PACK * HALF], BF16)
-            copy(
-                values[:].rearrange("p (c i j) -> p c j i", i=2, j=PACK),
-                w3_raw[:, :, HALF * h : HALF * (h + 1)].rearrange("p j (c i) -> p c j i", i=2),
-            )
-            return values
 
         def near_gather(t):
             if t == PACK - 1:
@@ -162,8 +148,7 @@ def tile_picked_scan2_none_p_kernel(
 
         def near_sum(t):
             nc.vector.tensor_tensor(b2_sb[t][:], near_term[t], b_sb[t], ADD)
-            c0 = HALF if t == PACK - 1 else 0
-            nc.sync.dma_start(out=b2_all[:, t, c0:S], in_=b2_sb[t][:, c0:S])
+            nc.sync.dma_start(out=b2_all[:, t, :], in_=b2_sb[t][:])
 
         def decay_product(t):
             nc.vector.tensor_tensor(a2_all[:, t, :], a_sb[t], a_near[t], MULT)
@@ -177,7 +162,6 @@ def tile_picked_scan2_none_p_kernel(
         near_sum(PACK - 1)
         for t in range(1, PACK):
             decay_product(t)
-        nc.vector.tensor_copy(b2_all[:, PACK - 1, 0:HALF], b2_sb[PACK - 1][:, 0:HALF])
 
         b2_far_head = tile("b2_far_head", [P, PACK, HALF], F32)
         b2_far_tail = tile("near_term3", [P, PACK, HALF], F32)
@@ -204,35 +188,42 @@ def tile_picked_scan2_none_p_kernel(
 
         out_rows = out.rearrange("(r p) s -> p r s", p=P)
 
-        def last_product(n):
+        def last_product(n, first_bank, rows_per_bank):
             c0, c1 = CHUNKS[n]
             quantize(z_codes, z_scales, c0, c1, z_bf[:, PACK * c0 : PACK * c1])
             res = keep.tile([P, PACK, c1 - c0], F32, name="res%d" % n)
-            for pair in range(2):
-                acc = psum.tile([P, 2, c1 - c0], F32, name="bank%d" % (1 + 2 * n + pair))
-                for r in range(2):
-                    product(acc[:, r, :], 2, 2 * pair + r, z_codes[:, c0:c1], z_scales[:, c0:c1])
-                rows = slice(2 * pair, 2 * pair + 2)
-                copy = nc.vector.tensor_copy if c1 == S and pair == 1 else nc.scalar.copy
-                queue = nc.scalar if c1 == S and pair == 0 else nc.sync
+            for r0 in range(0, PACK, rows_per_bank):
+                acc = psum.tile([P, rows_per_bank, c1 - c0], F32, name="bank%d" % (first_bank + r0 // rows_per_bank))
+                for r in range(rows_per_bank):
+                    product(acc[:, r, :], 2, r0 + r, z_codes[:, c0:c1], z_scales[:, c0:c1])
+                rows = slice(r0, r0 + rows_per_bank)
+                copy = nc.vector.tensor_copy if c1 == S and r0 else nc.scalar.copy
+                queue = nc.scalar if c1 == S and not r0 else nc.sync
                 copy(res[:, rows, :], acc[:])
                 queue.dma_start(out=out_rows[:, rows, c0:c1], in_=res[:, rows, :])
 
+        w3_bf = tile("b_window3", [P, PACK * N], BF16)
+
+        def cast_w3(c0, copy):
+            copy(
+                w3_bf[:, PACK * c0 : PACK * (c0 + HALF)].rearrange("p (c i j) -> p c j i", i=2, j=PACK),
+                w3_raw[:, :, c0 : c0 + HALF].rearrange("p j (c i) -> p c j i", i=2),
+            )
+
         far_gather(0)
-        w3_low = cast_w3(0, "near_term2", nc.vector.tensor_copy)
-        w3_high = cast_w3(1, "b_window3", nc.scalar.copy)
+        cast_w3(HALF, nc.scalar.copy)
         far_gather(1)
         far_gather(2)
         far_product(0)
-        quantize(w_codes[2], w_scales[2], 0, HALF, w3_low[:])
+        cast_w3(0, nc.vector.tensor_copy)
         far_sum(0)
-        quantize(w_codes[2], w_scales[2], HALF, N, w3_high[:])
+        quantize(w_codes[2], w_scales[2], 0, N, w3_bf[:])
         far_term_tail = tile("far_term", [P, PACK, HALF], F32)
         far_term.extend([far_term_tail[:, :, 0:P], far_term_tail[:, :, P:HALF]])
         far_product(1)
-        last_product(0)
+        last_product(0, 2, 2)
         far_sum(1)
         far_product(2)
-        last_product(1)
+        last_product(1, 4, 2)
         far_sum(2)
-        last_product(2)
+        last_product(2, 6, 2)

@@ -82,7 +82,7 @@ def tile_picked_scan2_none_p_kernel(
         nc.sync.dma_start(far_sb[:], far)
         load_weight(w3_raw, w3)
 
-        def cast_dealt(values, raw, m0, t0=0, t1=PACK):
+        def cast_dealt(values, raw, m0, t0, t1):
             dst = values[:].rearrange("p (t m j) -> p m j t", t=PACK, j=PACK)
             src = raw[:].rearrange("p j (m t) -> p m j t", t=PACK)
             nc.vector.tensor_copy(dst[:, m0 : m0 + src.shape[1], :, t0:t1], src[:, :, :, t0:t1])
@@ -124,7 +124,8 @@ def tile_picked_scan2_none_p_kernel(
             product(acc[:], 0, t, xw_pick[:, c0:c1], xs_pick[:, c0:c1])
             nc.scalar.activation(a_sb[t][:, c0:c1], acc[:], SIGMOID)
 
-        cast_dealt(w2_bf, w2_raw[0], 0)
+        cast_dealt(w2_bf, w2_raw[0], 0, 0, 2)
+        cast_dealt(w2_bf, w2_raw[0], 0, 2, PACK)
         cast_dealt(w2_bf, w2_raw[1], HALF // PACK, 0, 2)
         cast_dealt(w2_bf, w2_raw[1], HALF // PACK, 2, PACK)
         quantize(w_codes[1], w_scales[1], 0, P, w2_bf[:, 0:H])
@@ -153,14 +154,13 @@ def tile_picked_scan2_none_p_kernel(
         def decay_product(t):
             nc.vector.tensor_tensor(a2_all[:, t, :], a_sb[t], a_near[t], MULT)
 
-        a2_all = tile("a2_all", [P, PACK, S], F32)
         near_gather(0)
         for t in range(1, PACK):
             near_gather(t)
             near_sum(t - 1)
-        decay_product(0)
         near_sum(PACK - 1)
-        for t in range(1, PACK):
+        a2_all = tile("near_term2", [P, PACK, S], F32)
+        for t in range(PACK):
             decay_product(t)
 
         b2_far_head = tile("b2_far_head", [P, PACK, HALF], F32)
@@ -214,10 +214,10 @@ def tile_picked_scan2_none_p_kernel(
         cast_w3(HALF, nc.scalar.copy)
         far_gather(1)
         far_gather(2)
-        far_product(0)
         cast_w3(0, nc.vector.tensor_copy)
-        far_sum(0)
+        far_product(0)
         quantize(w_codes[2], w_scales[2], 0, N, w3_bf[:])
+        far_sum(0)
         far_term_tail = tile("far_term", [P, PACK, HALF], F32)
         far_term.extend([far_term_tail[:, :, 0:P], far_term_tail[:, :, P:HALF]])
         far_product(1)

@@ -115,6 +115,9 @@ def tile_picked_scan2_none_p_kernel(
         cast_dealt(w1_bf, w1_raw, 0, 2, PACK)
         quantize(w_codes[0], w_scales[0], 0, 2 * P, w1_bf[:, 0 : 2 * H])
         quantize(w_codes[0], w_scales[0], 2 * P, H, w1_bf[:, 2 * H : PACK * H])
+        warm = psum.tile([P, S], F32, name="bank6")
+        for t in range(2):
+            product(warm[:], 0, t, w_codes[0][:], w_scales[0][:])
         nc.vector.tensor_copy(xs_pick[:], xs[:].indirect(offs_sb[:]))
         for c0 in (0, HALF):
             nc.vector.tensor_copy(xw_pick[:, c0 : c0 + HALF], xw[:].bitcast(U32).indirect(offsets(offs_sb, c0, c0 + HALF)))

@@ -151,23 +151,32 @@ def tile_picked_scan2_none_p_kernel(
 
 
         def near_sum(t):
-            nc.vector.tensor_tensor(b2_sb[t][:], near_term[t], b_sb[t], ADD)
+            nc.vector.tensor_tensor(b2_sb[t][:], b_ps[t][:], near_term[t], ADD)
             nc.sync.dma_start(out=b2_all[:, t, :], in_=b2_sb[t][:])
 
         def decay_product(t):
             nc.vector.tensor_tensor(a2_all[:, t, :], a_sb[t], a_near[t], MULT)
 
-        near_gather(0)
-        for t in range(1, PACK):
+        for t in range(PACK - 1):
             near_gather(t)
-            near_sum(t - 1)
-        near_sum(PACK - 1)
+        w3_low = tile("b_window2", [P, PACK * HALF], BF16)
+        nc.gpsimd.tensor_scalar(
+            w3_low[:].rearrange("p (c i j) -> p c j i", i=PACK, j=PACK),
+            w3_raw[:, :, 0:HALF].rearrange("p j (c i) -> p c j i", i=PACK),
+            1.0, 0.0, MULT, ADD,
+        )
+        for t in range(PACK - 1):
+            near_sum(t)
+        near_gather(PACK - 1)
         a2_all = tile("near_term2", [P, PACK, S], F32)
-        for t in range(PACK):
+        decay_product(0)
+        near_sum(PACK - 1)
+        for t in range(1, PACK):
             decay_product(t)
 
         b2_far_head = tile("b2_far_head", [P, PACK, HALF], F32)
-        b2_far_tail = tile("near_term3", [P, PACK, HALF], F32)
+        held = tile("near_term3", [P, 6 * HALF], F32)
+        b2_far_tail = held[:, 0 : PACK * HALF].rearrange("p (t c) -> p t c", t=PACK)
         b2_far = [b2_far_head[:], b2_far_tail[:, :, 0:P], b2_far_tail[:, :, P:HALF]]
         far_term = [tile("far_term", [P, PACK, HALF], F32)[:]]
 
@@ -205,11 +214,11 @@ def tile_picked_scan2_none_p_kernel(
                 copy(res[:, rows, :], acc[:])
                 queue.dma_start(out=out_rows[:, rows, c0:c1], in_=res[:, rows, :])
 
-        w3_bf = tile("b_window3", [P, PACK * N], BF16)
+        w3_high = held[:, PACK * HALF : 6 * HALF].bitcast(BF16)
 
         def cast_w3(c0, copy):
             copy(
-                w3_bf[:, PACK * c0 : PACK * (c0 + HALF)].rearrange("p (c i j) -> p c j i", i=2, j=PACK),
+                w3_high.rearrange("p (c i j) -> p c j i", i=2, j=PACK),
                 w3_raw[:, :, c0 : c0 + HALF].rearrange("p j (c i) -> p c j i", i=2),
             )
 
@@ -217,9 +226,9 @@ def tile_picked_scan2_none_p_kernel(
         cast_w3(HALF, nc.scalar.copy)
         far_gather(1)
         far_gather(2)
-        cast_w3(0, nc.vector.tensor_copy)
+        quantize(w_codes[2], w_scales[2], 0, HALF, w3_low[:])
         far_product(0)
-        quantize(w_codes[2], w_scales[2], 0, N, w3_bf[:])
+        quantize(w_codes[2], w_scales[2], HALF, N, w3_high)
         far_sum(0)
         far_term_tail = tile("far_term", [P, PACK, HALF], F32)
         far_term.extend([far_term_tail[:, :, 0:P], far_term_tail[:, :, P:HALF]])

@@ -21,6 +21,7 @@ P = 128
 PACK = 4
 GROUP = 16
 HALF = 256
+W3_SPLIT = 384
 CHUNKS = ((0, HALF), (HALF, HALF + P), (HALF + P, S))
 
 
@@ -30,6 +31,7 @@ def tile_picked_scan2_none_p_kernel(
     nc = tc.nc
     with ExitStack() as ctx:
         keep = ctx.enter_context(tc.tile_pool(name="keep", bufs=1))
+        shared = ctx.enter_context(tc.tile_pool(name="shared", bufs=1))
         psum = ctx.enter_context(tc.psum_pool(name="psum", bufs=1))
 
         def tile(name, shape, dtype):
@@ -56,10 +58,11 @@ def tile_picked_scan2_none_p_kernel(
         b_window = tiles("b_window", [P, 2 * S], F32, PACK)
         a_sb = [w[:, 0:S] for w in a_window]
         b_sb = [w[:, 0:S] for w in b_window]
-        b2_sb = tiles("b2_sb", [P, S], F32, PACK)
         near_term = [t[:] for t in tiles("near_term", [P, S], F32, PACK)]
         a_near = [tile("a_near", [P, S], F32)[:]]
-        b_near = tile("b_near", [P, S], F32)[:]
+        b_near_tile = shared.tile([P, PACK * S], F32, name="b_near", offset=0)
+        b_near = b_near_tile[:, 0:S]
+        b2_sb = [shared.tile([P, S], F32, name="b2_sb%d" % t, offset=4 * S * t) for t in range(PACK)]
         b2_all = tile("b2_all", [P, PACK, S], F32)
         z_bf = tile("z_bf", [P, PACK * S], BF16)
         z_codes = tile("z_codes", [P, S], U32)
@@ -159,23 +162,22 @@ def tile_picked_scan2_none_p_kernel(
 
         for t in range(PACK - 1):
             near_gather(t)
-        w3_low = tile("b_window2", [P, PACK * HALF], BF16)
+        near_gather(PACK - 1)
+        a2_all = tile("b_window3", [P, PACK, S], F32)
+        decay_product(0)
+        w3_low = tile("a_near", [P, PACK * W3_SPLIT], BF16)
         nc.gpsimd.tensor_scalar(
-            w3_low[:].rearrange("p (c i j) -> p c j i", i=PACK, j=PACK),
-            w3_raw[:, :, 0:HALF].rearrange("p j (c i) -> p c j i", i=PACK),
+            w3_low[:].rearrange("p (c j) -> p c j", j=PACK),
+            w3_raw[:, :, 0:W3_SPLIT].rearrange("p j c -> p c j"),
             1.0, 0.0, MULT, ADD,
         )
-        for t in range(PACK - 1):
+        for t in range(PACK):
             near_sum(t)
-        near_gather(PACK - 1)
-        a2_all = tile("near_term2", [P, PACK, S], F32)
-        decay_product(0)
-        near_sum(PACK - 1)
         for t in range(1, PACK):
             decay_product(t)
 
         b2_far_head = tile("b2_far_head", [P, PACK, HALF], F32)
-        held = tile("near_term3", [P, 6 * HALF], F32)
+        held = tile("near_term3", [P, 5 * HALF], F32)
         b2_far_tail = held[:, 0 : PACK * HALF].rearrange("p (t c) -> p t c", t=PACK)
         b2_far = [b2_far_head[:], b2_far_tail[:, :, 0:P], b2_far_tail[:, :, P:HALF]]
         far_term = [tile("far_term", [P, PACK, HALF], F32)[:]]
@@ -214,21 +216,21 @@ def tile_picked_scan2_none_p_kernel(
                 copy(res[:, rows, :], acc[:])
                 queue.dma_start(out=out_rows[:, rows, c0:c1], in_=res[:, rows, :])
 
-        w3_high = held[:, PACK * HALF : 6 * HALF].bitcast(BF16)
+        w3_high = held[:, PACK * HALF : 5 * HALF].bitcast(BF16)
 
         def cast_w3(c0, copy):
             copy(
                 w3_high.rearrange("p (c i j) -> p c j i", i=2, j=PACK),
-                w3_raw[:, :, c0 : c0 + HALF].rearrange("p j (c i) -> p c j i", i=2),
+                w3_raw[:, :, c0:N].rearrange("p j (c i) -> p c j i", i=2),
             )
 
         far_gather(0)
-        cast_w3(HALF, nc.scalar.copy)
+        cast_w3(W3_SPLIT, nc.scalar.copy)
         far_gather(1)
         far_gather(2)
-        quantize(w_codes[2], w_scales[2], 0, HALF, w3_low[:])
+        quantize(w_codes[2], w_scales[2], 0, W3_SPLIT, w3_low[:])
         far_product(0)
-        quantize(w_codes[2], w_scales[2], HALF, N, w3_high)
+        quantize(w_codes[2], w_scales[2], W3_SPLIT, N, w3_high)
         far_sum(0)
         far_term_tail = tile("far_term", [P, PACK, HALF], F32)
         far_term.extend([far_term_tail[:, :, 0:P], far_term_tail[:, :, P:HALF]])

@@ -21,7 +21,7 @@ P = 128
 PACK = 4
 GROUP = 16
 HALF = 256
-W3_SPLIT = 384
+W3_SPLIT = 128
 CHUNKS = ((0, HALF), (HALF, HALF + P), (HALF + P, S))
 
 
@@ -32,6 +32,7 @@ def tile_picked_scan2_none_p_kernel(
     with ExitStack() as ctx:
         keep = ctx.enter_context(tc.tile_pool(name="keep", bufs=1))
         shared = ctx.enter_context(tc.tile_pool(name="shared", bufs=1))
+        late = ctx.enter_context(tc.tile_pool(name="late", bufs=1))
         psum = ctx.enter_context(tc.psum_pool(name="psum", bufs=1))
 
         def tile(name, shape, dtype):
@@ -51,18 +52,19 @@ def tile_picked_scan2_none_p_kernel(
         w1_raw = tile("w1_raw", [P, PACK, H], F32)
         w2_raw = tiles("w2_raw", [P, PACK, HALF], F32, 2)
         w3_raw = tile("w3_raw", [P, PACK, N], F32)
-        w_codes = tiles("w_codes", [P, H], U32, 3)
+        w_codes = tiles("w_codes", [P, H], U32, 2)
         w_scales = tiles("w_scales", [P, H], U8, 3)
 
         a_window = tiles("a_window", [P, 2 * S], F32, PACK)
-        b_window = tiles("b_window", [P, 2 * S], F32, PACK)
+        b_window = tiles("b_window", [P, 2 * S], F32, PACK - 1)
+        b_window.insert(2, shared.tile([P, PACK * S], F32, name="b_third", offset=0))
         a_sb = [w[:, 0:S] for w in a_window]
         b_sb = [w[:, 0:S] for w in b_window]
+        b2_sb = [shared.tile([P, S], F32, name="b2_sb%d" % t, offset=4 * S * t) for t in range(PACK - 1)]
+        b2_sb.append(tile("b2_last", [P, S], F32))
+        a2_all = shared.tile([P, PACK, S], F32, name="a2_all", offset=4 * S * (PACK - 1))
         near_term = [t[:] for t in tiles("near_term", [P, S], F32, PACK)]
         a_near = [tile("a_near", [P, S], F32)[:]]
-        b_near_tile = shared.tile([P, PACK * S], F32, name="b_near", offset=0)
-        b_near = b_near_tile[:, 0:S]
-        b2_sb = [shared.tile([P, S], F32, name="b2_sb%d" % t, offset=4 * S * t) for t in range(PACK)]
         b2_all = tile("b2_all", [P, PACK, S], F32)
         z_bf = tile("z_bf", [P, PACK * S], BF16)
         z_codes = tile("z_codes", [P, S], U32)
@@ -142,45 +144,36 @@ def tile_picked_scan2_none_p_kernel(
             nc.scalar.copy(b_sb[t], b_ps[t][:])
 
         a_near.extend(tile(name, [P, S], F32)[:] for name in ("w_codes1", "w_scales1", "xw_pick"))
-        nc.scalar.activation(b_near, b_window[PACK - 1][:].indirect(near_sb[:]), COPY)
         for t in range(1, PACK):
             nc.scalar.activation(a_near[t], a_window[t][:].indirect(near_sb[:]), COPY)
 
         def near_gather(t):
-            if t == PACK - 1:
-                nc.vector.tensor_tensor(near_term[t], b_near, a_sb[t], MULT)
-            else:
-                nc.vector.tensor_tensor(near_term[t], b_window[t][:].indirect(near_sb[:]), a_sb[t], MULT)
-
+            nc.vector.tensor_tensor(near_term[t], b_window[t][:].indirect(near_sb[:]), a_sb[t], MULT)
 
         def near_sum(t):
             nc.vector.tensor_tensor(b2_sb[t][:], b_ps[t][:], near_term[t], ADD)
             nc.sync.dma_start(out=b2_all[:, t, :], in_=b2_sb[t][:])
 
-        def decay_product(t):
-            nc.vector.tensor_tensor(a2_all[:, t, :], a_sb[t], a_near[t], MULT)
+        def decay_product(t, engine):
+            engine.tensor_tensor(a2_all[:, t, :], a_sb[t], a_near[t], MULT)
 
-        for t in range(PACK - 1):
+        for t in range(PACK):
             near_gather(t)
-        near_gather(PACK - 1)
-        a2_all = tile("b_window3", [P, PACK, S], F32)
-        decay_product(0)
-        w3_low = tile("a_near", [P, PACK * W3_SPLIT], BF16)
-        nc.gpsimd.tensor_scalar(
-            w3_low[:].rearrange("p (c j) -> p c j", j=PACK),
-            w3_raw[:, :, 0:W3_SPLIT].rearrange("p j c -> p c j"),
-            1.0, 0.0, MULT, ADD,
-        )
+        for t in range(2):
+            decay_product(t, nc.gpsimd)
         for t in range(PACK):
             near_sum(t)
-        for t in range(1, PACK):
-            decay_product(t)
+        for t in range(2, PACK):
+            decay_product(t, nc.vector)
 
         b2_far_head = tile("b2_far_head", [P, PACK, HALF], F32)
-        held = tile("near_term3", [P, 5 * HALF], F32)
+        held = tile("near_term3", [P, PACK * HALF + 2 * N], F32)
         b2_far_tail = held[:, 0 : PACK * HALF].rearrange("p (t c) -> p t c", t=PACK)
         b2_far = [b2_far_head[:], b2_far_tail[:, :, 0:P], b2_far_tail[:, :, P:HALF]]
-        far_term = [tile("far_term", [P, PACK, HALF], F32)[:]]
+        far_term_head = late.tile([P, PACK, HALF], F32, name="far_term_head", offset=2048, align_bytes=64)
+        far_term_tail = late.tile([P, PACK, HALF], F32, name="far_term_tail", offset=0, align_bytes=64)
+        w_codes.append(late.tile([P, H], U32, name="w3_codes", offset=4096, align_bytes=64))
+        far_term = [far_term_head[:], far_term_tail[:, :, 0:P], far_term_tail[:, :, P:HALF]]
 
         def far_gather(n):
             c0, c1 = CHUNKS[n]
@@ -216,24 +209,22 @@ def tile_picked_scan2_none_p_kernel(
                 copy(res[:, rows, :], acc[:])
                 queue.dma_start(out=out_rows[:, rows, c0:c1], in_=res[:, rows, :])
 
-        w3_high = held[:, PACK * HALF : 5 * HALF].bitcast(BF16)
+        w3_bf = held[:, PACK * HALF : PACK * HALF + 2 * N].bitcast(BF16)
 
-        def cast_w3(c0, copy):
+        def cast_w3(c0, c1, copy):
             copy(
-                w3_high.rearrange("p (c i j) -> p c j i", i=2, j=PACK),
-                w3_raw[:, :, c0:N].rearrange("p j (c i) -> p c j i", i=2),
+                w3_bf[:, PACK * c0 : PACK * c1].rearrange("p (c i j) -> p c j i", i=2, j=PACK),
+                w3_raw[:, :, c0:c1].rearrange("p j (c i) -> p c j i", i=2),
             )
 
         far_gather(0)
-        cast_w3(W3_SPLIT, nc.scalar.copy)
+        cast_w3(W3_SPLIT, N, nc.scalar.copy)
         far_gather(1)
         far_gather(2)
-        quantize(w_codes[2], w_scales[2], 0, W3_SPLIT, w3_low[:])
         far_product(0)
-        quantize(w_codes[2], w_scales[2], W3_SPLIT, N, w3_high)
+        cast_w3(0, W3_SPLIT, nc.vector.tensor_copy)
         far_sum(0)
-        far_term_tail = tile("far_term", [P, PACK, HALF], F32)
-        far_term.extend([far_term_tail[:, :, 0:P], far_term_tail[:, :, P:HALF]])
+        quantize(w_codes[2], w_scales[2], 0, N, w3_bf)
         far_product(1)
         last_product(0, 2, 2)
         far_sum(1)

@@ -167,9 +167,7 @@ def tile_picked_scan2_none_p_kernel(
             decay_product(t, nc.vector)
 
         b2_far_head = tile("b2_far_head", [P, PACK, HALF], F32)
-        held = tile("near_term3", [P, PACK * HALF + 2 * N], F32)
-        b2_far_tail = held[:, 0 : PACK * HALF].rearrange("p (t c) -> p t c", t=PACK)
-        b2_far = [b2_far_head[:], b2_far_tail[:, :, 0:P], b2_far_tail[:, :, P:HALF]]
+        b2_far = [b2_far_head[:], tile("near_term3", [P, PACK, P], F32)[:]]
         far_term_head = late.tile([P, PACK, HALF], F32, name="far_term_head", offset=2048, align_bytes=64)
         far_term_tail = late.tile([P, PACK, HALF], F32, name="far_term_tail", offset=0, align_bytes=64)
         w_codes.append(late.tile([P, H], U32, name="w3_codes", offset=4096, align_bytes=64))
@@ -180,9 +178,9 @@ def tile_picked_scan2_none_p_kernel(
             for t in range(PACK):
                 nc.scalar.activation(b2_far[n][:, t, :], b2_sb[t][:].indirect(offsets(far_sb, c0, c1)), COPY)
 
-        def far_product(n):
+        def far_product(n, t0=0, t1=PACK):
             c0, c1 = CHUNKS[n]
-            nc.vector.tensor_tensor(far_term[n], b2_far[n], a2_all[:, :, c0:c1], MULT)
+            nc.vector.tensor_tensor(far_term[n][:, t0:t1, :], b2_far[n][:, t0:t1, :], a2_all[:, t0:t1, c0:c1], MULT)
 
         def far_sum(n):
             c0, c1 = CHUNKS[n]
@@ -193,42 +191,59 @@ def tile_picked_scan2_none_p_kernel(
                 ADD,
             )
 
+        def quantize_z(n):
+            c0, c1 = CHUNKS[n]
+            quantize(z_codes, z_scales, c0, c1, z_bf[:, PACK * c0 : PACK * c1])
+
         out_rows = out.rearrange("(r p) s -> p r s", p=P)
 
         def last_product(n, first_bank, rows_per_bank):
             c0, c1 = CHUNKS[n]
-            quantize(z_codes, z_scales, c0, c1, z_bf[:, PACK * c0 : PACK * c1])
             res = keep.tile([P, PACK, c1 - c0], F32, name="res%d" % n)
             for r0 in range(0, PACK, rows_per_bank):
                 acc = psum.tile([P, rows_per_bank, c1 - c0], F32, name="bank%d" % (first_bank + r0 // rows_per_bank))
                 for r in range(rows_per_bank):
                     product(acc[:, r, :], 2, r0 + r, z_codes[:, c0:c1], z_scales[:, c0:c1])
                 rows = slice(r0, r0 + rows_per_bank)
-                copy = nc.vector.tensor_copy if c1 == S and r0 else nc.scalar.copy
-                queue = nc.scalar if c1 == S and not r0 else nc.sync
-                copy(res[:, rows, :], acc[:])
-                queue.dma_start(out=out_rows[:, rows, c0:c1], in_=res[:, rows, :])
+                nc.scalar.copy(res[:, rows, :], acc[:])
+                nc.sync.dma_start(out=out_rows[:, rows, c0:c1], in_=res[:, rows, :])
 
-        w3_bf = held[:, PACK * HALF : PACK * HALF + 2 * N].bitcast(BF16)
+        def last_chunk(n, banks):
+            c0, c1 = CHUNKS[n]
+            res = tiles("res_last", [P, c1 - c0], F32, PACK)
+            for r in range(PACK):
+                acc = psum.tile([P, c1 - c0], F32, name="bank%d" % banks[r])
+                product(acc[:], 2, r, z_codes[:, c0:c1], z_scales[:, c0:c1])
+                copy = nc.scalar.copy if r % 2 else nc.vector.tensor_copy
+                copy(res[r][:], acc[:])
+                queue = nc.scalar if r == PACK - 1 else nc.sync
+                queue.dma_start(out=out_rows[:, r, c0:c1], in_=res[r][:])
 
-        def cast_w3(c0, c1, copy):
+
+        def cast_w3(w3_bf, c0, c1, copy):
             copy(
                 w3_bf[:, PACK * c0 : PACK * c1].rearrange("p (c i j) -> p c j i", i=2, j=PACK),
                 w3_raw[:, :, c0:c1].rearrange("p j (c i) -> p c j i", i=2),
             )
 
         far_gather(0)
-        cast_w3(W3_SPLIT, N, nc.scalar.copy)
         far_gather(1)
+        far_product(0, 0, 2)
+        far_product(0, 2, PACK)
+        w3_bf = tile("b2_far_head", [P, PACK * N], BF16)[:]
+        cast_w3(w3_bf, 0, W3_SPLIT, nc.vector.tensor_copy)
+        cast_w3(w3_bf, W3_SPLIT, N, nc.scalar.copy)
+        b2_far.append(tile("w3_raw", [P, PACK, P], F32)[:])
         far_gather(2)
-        far_product(0)
-        cast_w3(0, W3_SPLIT, nc.vector.tensor_copy)
         far_sum(0)
-        quantize(w_codes[2], w_scales[2], 0, N, w3_bf)
         far_product(1)
-        last_product(0, 2, 2)
+        quantize_z(0)
+        quantize(w_codes[2], w_scales[2], 0, N, w3_bf)
+        last_product(0, 2, 1)
         far_sum(1)
         far_product(2)
-        last_product(1, 4, 2)
+        quantize_z(1)
+        last_product(1, 6, 2)
         far_sum(2)
-        last_product(2, 6, 2)
+        quantize_z(2)
+        last_chunk(2, (0, 1, 2, 3))

@@ -206,7 +206,9 @@ def tile_picked_scan2_none_p_kernel(
                     product(acc[:, r, :], 2, r0 + r, z_codes[:, c0:c1], z_scales[:, c0:c1])
                 rows = slice(r0, r0 + rows_per_bank)
                 nc.scalar.copy(res[:, rows, :], acc[:])
-                nc.sync.dma_start(out=out_rows[:, rows, c0:c1], in_=res[:, rows, :])
+                if rows.stop % 2 == 0:
+                    pair = slice(rows.stop - 2, rows.stop)
+                    nc.sync.dma_start(out=out_rows[:, pair, c0:c1], in_=res[:, pair, :])
 
         def last_chunk(n, banks):
             c0, c1 = CHUNKS[n]

@@ -120,9 +120,6 @@ def tile_picked_scan2_none_p_kernel(
         cast_dealt(w1_bf, w1_raw, 0, 2, PACK)
         quantize(w_codes[0], w_scales[0], 0, 2 * P, w1_bf[:, 0 : 2 * H])
         quantize(w_codes[0], w_scales[0], 2 * P, H, w1_bf[:, 2 * H : PACK * H])
-        warm = psum.tile([P, S], F32, name="bank6")
-        for t in range(2):
-            product(warm[:], 0, t, w_codes[0][:], w_scales[0][:])
         nc.vector.tensor_copy(xs_pick[:], xs[:].indirect(offs_sb[:]))
         for c0 in (0, HALF):
             nc.vector.tensor_copy(xw_pick[:, c0 : c0 + HALF], xw[:].bitcast(U32).indirect(offsets(offs_sb, c0, c0 + HALF)))

@@ -21,7 +21,6 @@ P = 128
 PACK = 4
 GROUP = 16
 HALF = 256
-W3_SPLIT = 128
 CHUNKS = ((0, HALF), (HALF, HALF + P), (HALF + P, S))
 
 
@@ -51,8 +50,8 @@ def tile_picked_scan2_none_p_kernel(
 
         w1_raw = tile("w1_raw", [P, PACK, H], F32)
         w2_raw = tiles("w2_raw", [P, PACK, HALF], F32, 2)
-        w3_raw = tile("w3_raw", [P, PACK, N], F32)
-        w_codes = tiles("w_codes", [P, H], U32, 2)
+        w3_raw = tiles("w3_raw", [P, PACK, HALF], F32, 2)
+        w_codes = tiles("w_codes", [P, H], U32, 3)
         w_scales = tiles("w_scales", [P, H], U8, 3)
 
         a_window = tiles("a_window", [P, 2 * S], F32, PACK)
@@ -63,8 +62,8 @@ def tile_picked_scan2_none_p_kernel(
         b2_sb = [shared.tile([P, S], F32, name="b2_sb%d" % t, offset=4 * S * t) for t in range(PACK - 1)]
         b2_sb.append(tile("b2_last", [P, S], F32))
         a2_all = shared.tile([P, PACK, S], F32, name="a2_all", offset=4 * S * (PACK - 1))
-        near_term = [t[:] for t in tiles("near_term", [P, S], F32, PACK)]
-        a_near = [tile("a_near", [P, S], F32)[:]]
+        near_term = [t[:] for t in tiles("near_term", [P, S], F32, PACK - 1)]
+        near_term.append(late.tile([P, S], F32, name="near_last", offset=1024, align_bytes=64)[:])
         b2_all = tile("b2_all", [P, PACK, S], F32)
         z_bf = tile("z_bf", [P, PACK * S], BF16)
         z_codes = tile("z_codes", [P, S], U32)
@@ -83,9 +82,10 @@ def tile_picked_scan2_none_p_kernel(
         nc.sync.dma_start(out=xw[:], in_=x_words[0].rearrange("p n t -> p (n t)").bitcast(I32))
         load_weight(w2_raw[0], w2[:, 0:HALF])
         load_weight(w2_raw[1], w2[:, HALF:H])
+        load_weight(w3_raw[0], w3[:, 0:HALF])
+        load_weight(w3_raw[1], w3[:, HALF:N])
         nc.sync.dma_start(near_sb[:], near)
         nc.sync.dma_start(far_sb[:], far)
-        load_weight(w3_raw, w3)
 
         def cast_dealt(values, raw, m0, t0, t1):
             dst = values[:].rearrange("p (t m j) -> p m j t", t=PACK, j=PACK)
@@ -97,9 +97,10 @@ def tile_picked_scan2_none_p_kernel(
 
         def product(acc, i, tile_no, codes, scales):
             cols = slice(P * tile_no, P * (tile_no + 1))
+            held = w_codes[3] if i == 2 and tile_no >= 2 else w_codes[i]
             nc.tensor.matmul_mx(
                 out=acc,
-                lhsT=w_codes[i][:, cols].bitcast(FP8X4),
+                lhsT=held[:, cols].bitcast(FP8X4),
                 lhsT_scale=w_scales[i][:, cols],
                 rhs=codes.bitcast(FP8X4),
                 rhs_scale=scales,
@@ -136,20 +137,32 @@ def tile_picked_scan2_none_p_kernel(
         quantize(w_codes[1], w_scales[1], 0, P, w2_bf[:, 0:H])
         quantize(w_codes[1], w_scales[1], P, H, w2_bf[:, H : PACK * H])
         b_ps = [first_product(1, t, (6 + t) % 8) for t in range(PACK)]
-        nc.vector.tensor_copy(a_near[0], a_window[0][:].indirect(near_sb[:]))
+
+        def cast_w3(w3_bf, h, c0, c1, copy):
+            copy(
+                w3_bf[:, PACK * c0 : PACK * c1].rearrange("p (c i j) -> p c j i", i=2, j=PACK),
+                w3_raw[h][:, :, c0:c1].rearrange("p j (c i) -> p c j i", i=2),
+            )
+
+        w3_bf = tiles("w3_bf", [P, PACK * HALF], BF16, 2)
+        for h in range(2):
+            cast_w3(w3_bf[h], h, 0, HALF, nc.vector.tensor_copy)
+        quantize(w_codes[2], w_scales[2], 0, HALF, w3_bf[0][:])
         for t in range(PACK):
             nc.scalar.copy(b_sb[t], b_ps[t][:])
 
-        a_near.extend(tile(name, [P, S], F32)[:] for name in ("w_codes1", "w_scales1", "xw_pick"))
-        for t in range(1, PACK):
+        a_near = [tile(name, [P, S], F32)[:] for name in ("w_codes1", "w_scales1", "xw_pick", "xs_pick")]
+        for t in range(PACK - 1):
             nc.scalar.activation(a_near[t], a_window[t][:].indirect(near_sb[:]), COPY)
+        nc.scalar.activation(a_near[3][:, 0:HALF], a_window[3][:].indirect(offsets(near_sb, 0, HALF)), COPY)
 
         def near_gather(t):
             nc.vector.tensor_tensor(near_term[t], b_window[t][:].indirect(near_sb[:]), a_sb[t], MULT)
 
         def near_sum(t):
             nc.vector.tensor_tensor(b2_sb[t][:], b_ps[t][:], near_term[t], ADD)
-            nc.sync.dma_start(out=b2_all[:, t, :], in_=b2_sb[t][:])
+            for c0, c1 in ((0, HALF), (HALF, S)) if t == PACK - 1 else ((0, S),):
+                nc.sync.dma_start(out=b2_all[:, t, c0:c1], in_=b2_sb[t][:, c0:c1])
 
         def decay_product(t, engine):
             engine.tensor_tensor(a2_all[:, t, :], a_sb[t], a_near[t], MULT)
@@ -160,14 +173,13 @@ def tile_picked_scan2_none_p_kernel(
             decay_product(t, nc.gpsimd)
         for t in range(PACK):
             near_sum(t)
-        for t in range(2, PACK):
-            decay_product(t, nc.vector)
+        decay_product(2, nc.vector)
+        nc.vector.tensor_tensor(a2_all[:, 3, 0:HALF], a_sb[3][:, 0:HALF], a_near[3][:, 0:HALF], MULT)
 
         b2_far_head = tile("b2_far_head", [P, PACK, HALF], F32)
-        b2_far = [b2_far_head[:], tile("near_term3", [P, PACK, P], F32)[:]]
-        far_term_head = late.tile([P, PACK, HALF], F32, name="far_term_head", offset=2048, align_bytes=64)
-        far_term_tail = late.tile([P, PACK, HALF], F32, name="far_term_tail", offset=0, align_bytes=64)
-        w_codes.append(late.tile([P, H], U32, name="w3_codes", offset=4096, align_bytes=64))
+        b2_far = [b2_far_head[:], late.tile([P, PACK, P], F32, name="b2_far_mid", offset=2048, align_bytes=64)[:]]
+        far_term_head = late.tile([P, PACK, HALF], F32, name="far_term_head", offset=4096, align_bytes=64)
+        far_term_tail = late.tile([P, PACK, HALF], F32, name="far_term_tail", offset=4096, align_bytes=64)
         far_term = [far_term_head[:], far_term_tail[:, :, 0:P], far_term_tail[:, :, P:HALF]]
 
         def far_gather(n):
@@ -218,26 +230,20 @@ def tile_picked_scan2_none_p_kernel(
                 queue = nc.scalar if r == PACK - 1 else nc.sync
                 queue.dma_start(out=out_rows[:, r, c0:c1], in_=res[r][:])
 
-
-        def cast_w3(w3_bf, c0, c1, copy):
-            copy(
-                w3_bf[:, PACK * c0 : PACK * c1].rearrange("p (c i j) -> p c j i", i=2, j=PACK),
-                w3_raw[:, :, c0:c1].rearrange("p j (c i) -> p c j i", i=2),
-            )
-
         far_gather(0)
+        a_near_late = late.tile([P, HALF], F32, name="a_near_late", offset=1024, align_bytes=64)
+        nc.scalar.activation(a_near_late[:], a_window[3][:].indirect(offsets(near_sb, HALF, S)), COPY)
         far_gather(1)
         far_product(0, 0, 2)
+        w_codes.append(tile("xw_pick", [P, N], U32))
+        quantize(w_codes[3], w_scales[2], HALF, N, w3_bf[1][:])
         far_product(0, 2, PACK)
-        w3_bf = tile("b2_far_head", [P, PACK * N], BF16)[:]
-        cast_w3(w3_bf, 0, W3_SPLIT, nc.vector.tensor_copy)
-        cast_w3(w3_bf, W3_SPLIT, N, nc.scalar.copy)
-        b2_far.append(tile("w3_raw", [P, PACK, P], F32)[:])
+        b2_far.append(tile("b2_far_head", [P, PACK, P], F32)[:])
         far_gather(2)
+        nc.vector.tensor_tensor(a2_all[:, 3, HALF:S], a_sb[3][:, HALF:S], a_near_late[:], MULT)
         far_sum(0)
         far_product(1)
         quantize_z(0)
-        quantize(w_codes[2], w_scales[2], 0, N, w3_bf)
         last_product(0, 2, 1)
         far_sum(1)
         far_product(2)

@@ -161,8 +161,8 @@ def tile_picked_scan2_none_p_kernel(
 
         def near_sum(t):
             nc.vector.tensor_tensor(b2_sb[t][:], b_ps[t][:], near_term[t], ADD)
-            for c0, c1 in ((0, HALF), (HALF, S)) if t == PACK - 1 else ((0, S),):
-                nc.sync.dma_start(out=b2_all[:, t, c0:c1], in_=b2_sb[t][:, c0:c1])
+            first = HALF if t == PACK - 1 else 0
+            nc.sync.dma_start(out=b2_all[:, t, first:S], in_=b2_sb[t][:, first:S])
 
         def decay_product(t, engine):
             engine.tensor_tensor(a2_all[:, t, :], a_sb[t], a_near[t], MULT)
@@ -173,14 +173,15 @@ def tile_picked_scan2_none_p_kernel(
             decay_product(t, nc.gpsimd)
         for t in range(PACK):
             near_sum(t)
+        nc.vector.tensor_tensor(b2_all[:, 3, 0:HALF], b_ps[3][:, 0:HALF], near_term[3][:, 0:HALF], ADD)
         decay_product(2, nc.vector)
         nc.vector.tensor_tensor(a2_all[:, 3, 0:HALF], a_sb[3][:, 0:HALF], a_near[3][:, 0:HALF], MULT)
 
         b2_far_head = tile("b2_far_head", [P, PACK, HALF], F32)
         b2_far = [b2_far_head[:], late.tile([P, PACK, P], F32, name="b2_far_mid", offset=2048, align_bytes=64)[:]]
         far_term_head = late.tile([P, PACK, HALF], F32, name="far_term_head", offset=4096, align_bytes=64)
-        far_term_tail = late.tile([P, PACK, HALF], F32, name="far_term_tail", offset=4096, align_bytes=64)
-        far_term = [far_term_head[:], far_term_tail[:, :, 0:P], far_term_tail[:, :, P:HALF]]
+        far_term_tail = late.tile([P, PACK, P], F32, name="far_term_tail", offset=4096, align_bytes=64)
+        far_term = [far_term_head[:], tile("far_term_mid", [P, PACK, P], F32)[:], far_term_tail[:]]
 
         def far_gather(n):
             c0, c1 = CHUNKS[n]
@@ -215,20 +216,19 @@ def tile_picked_scan2_none_p_kernel(
                     product(acc[:, r, :], 2, r0 + r, z_codes[:, c0:c1], z_scales[:, c0:c1])
                 rows = slice(r0, r0 + rows_per_bank)
                 nc.scalar.copy(res[:, rows, :], acc[:])
-                if rows.stop % 2 == 0:
-                    pair = slice(rows.stop - 2, rows.stop)
-                    nc.sync.dma_start(out=out_rows[:, pair, c0:c1], in_=res[:, pair, :])
+                nc.sync.dma_start(out=out_rows[:, rows, c0:c1], in_=res[:, rows, :])
 
         def last_chunk(n, banks):
             c0, c1 = CHUNKS[n]
-            res = tiles("res_last", [P, c1 - c0], F32, PACK)
+            res = tiles("res_last", [P, 2, c1 - c0], F32, 2)
             for r in range(PACK):
                 acc = psum.tile([P, c1 - c0], F32, name="bank%d" % banks[r])
                 product(acc[:], 2, r, z_codes[:, c0:c1], z_scales[:, c0:c1])
                 copy = nc.scalar.copy if r % 2 else nc.vector.tensor_copy
-                copy(res[r][:], acc[:])
-                queue = nc.scalar if r == PACK - 1 else nc.sync
-                queue.dma_start(out=out_rows[:, r, c0:c1], in_=res[r][:])
+                copy(res[r // 2][:, r % 2, :], acc[:])
+                if r % 2:
+                    queue = nc.scalar if r == PACK - 1 else nc.sync
+                    queue.dma_start(out=out_rows[:, r - 1 : r + 1, c0:c1], in_=res[r // 2][:])
 
         far_gather(0)
         a_near_late = late.tile([P, HALF], F32, name="a_near_late", offset=1024, align_bytes=64)

@@ -65,7 +65,7 @@ def tile_picked_scan2_none_p_kernel(
         near_term = [t[:] for t in tiles("near_term", [P, S], F32, PACK - 1)]
         near_term.append(late.tile([P, S], F32, name="near_last", offset=1024, align_bytes=64)[:])
         b2_all = tile("b2_all", [P, PACK, S], F32)
-        z_bf = tile("z_bf", [P, PACK * S], BF16)
+        z_bf = [tile(name, [P, PACK * (c1 - c0)], BF16) for name, (c0, c1) in zip(("z_first", "z_mid", "z_last"), CHUNKS)]
         z_codes = tile("z_codes", [P, S], U32)
         z_scales = tile("z_scales", [P, S], U8)
 
@@ -195,7 +195,7 @@ def tile_picked_scan2_none_p_kernel(
         def far_sum(n):
             c0, c1 = CHUNKS[n]
             nc.vector.tensor_tensor(
-                z_bf[:, PACK * c0 : PACK * c1].rearrange("p (c i t) -> p c t i", i=2, t=PACK),
+                z_bf[n][:].rearrange("p (c i t) -> p c t i", i=2, t=PACK),
                 far_term[n].rearrange("p t (c i) -> p c t i", i=2),
                 b2_all[:, :, c0:c1].rearrange("p t (c i) -> p c t i", i=2),
                 ADD,
@@ -203,11 +203,11 @@ def tile_picked_scan2_none_p_kernel(
 
         def quantize_z(n):
             c0, c1 = CHUNKS[n]
-            quantize(z_codes, z_scales, c0, c1, z_bf[:, PACK * c0 : PACK * c1])
+            quantize(z_codes, z_scales, c0, c1, z_bf[n][:])
 
         out_rows = out.rearrange("(r p) s -> p r s", p=P)
 
-        def last_product(n, first_bank, rows_per_bank):
+        def last_product(n, first_bank, rows_per_bank, last_copy=nc.scalar.copy):
             c0, c1 = CHUNKS[n]
             res = keep.tile([P, PACK, c1 - c0], F32, name="res%d" % n)
             for r0 in range(0, PACK, rows_per_bank):
@@ -215,6 +215,8 @@ def tile_picked_scan2_none_p_kernel(
                 for r in range(rows_per_bank):
                     product(acc[:, r, :], 2, r0 + r, z_codes[:, c0:c1], z_scales[:, c0:c1])
                 rows = slice(r0, r0 + rows_per_bank)
+                if rows.stop == PACK and last_copy is None:
+                    return res, rows, acc
                 nc.scalar.copy(res[:, rows, :], acc[:])
                 nc.sync.dma_start(out=out_rows[:, rows, c0:c1], in_=res[:, rows, :])
 
@@ -248,7 +250,10 @@ def tile_picked_scan2_none_p_kernel(
         far_sum(1)
         far_product(2)
         quantize_z(1)
-        last_product(1, 6, 2)
+        res, rows, acc = last_product(1, 6, 2, None)
         far_sum(2)
         quantize_z(2)
+        res = tile("z_last", [P, 2, P], F32)
+        nc.vector.tensor_copy(res[:], acc[:])
+        nc.sync.dma_start(out=out_rows[:, rows, CHUNKS[1][0] : CHUNKS[1][1]], in_=res[:])
         last_chunk(2, (0, 1, 2, 3))

from contextlib import ExitStack

import concourse.mybir as mybir

K, T, S, H, N = 512, 2048, 512, 512, 512
FLOPS = 2 * K * H * S * 2 + 2 * H * N * S

F32 = mybir.dt.float32
BF16 = mybir.dt.bfloat16
I32 = mybir.dt.int32
U32 = mybir.dt.uint32
U16 = mybir.dt.uint16
U8 = mybir.dt.uint8
FP8X4 = mybir.dt.float8_e4m3fn_x4
MULT = mybir.AluOpType.mult
ADD = mybir.AluOpType.add
SIGMOID = mybir.ActivationFunctionType.Sigmoid
COPY = mybir.ActivationFunctionType.Copy

P = 128
PACK = 4
GROUP = 16
HALF = 256
CHUNKS = ((0, HALF), (HALF, HALF + P), (HALF + P, S))


def tile_picked_scan2_none_p_kernel(
    tc, x_words, x_scales, w1, w2, w3, offs, near, far, out
):
    nc = tc.nc
    with ExitStack() as ctx:
        keep = ctx.enter_context(tc.tile_pool(name="keep", bufs=1))
        shared = ctx.enter_context(tc.tile_pool(name="shared", bufs=1))
        late = ctx.enter_context(tc.tile_pool(name="late", bufs=1))
        psum = ctx.enter_context(tc.psum_pool(name="psum", bufs=1))

        def tile(name, shape, dtype):
            return keep.tile(shape, dtype, name=name, align_bytes=64)

        def tiles(name, shape, dtype, count):
            return [tile("%s%d" % (name, i), shape, dtype) for i in range(count)]

        offs_sb = keep.tile([P, S // GROUP], U16, name="offs_sb")
        near_sb = keep.tile([P, S // GROUP], U16, name="near_sb")
        far_sb = keep.tile([P, S // GROUP], U16, name="far_sb")
        xw = tile("xw", [P, T], I32)
        xs = tile("xs", [P, T], U8)
        xw_pick = tile("xw_pick", [P, S], U32)
        xs_pick = tile("xs_pick", [P, S], U8)

        w1_raw = tile("w1_raw", [P, PACK, H], F32)
        w2_raw = tiles("w2_raw", [P, PACK, HALF], F32, 2)
        w3_raw = tiles("w3_raw", [P, PACK, HALF], F32, 2)
        w_codes = tiles("w_codes", [P, H], U32, 3)
        w_scales = tiles("w_scales", [P, H], U8, 3)

        a_window = tiles("a_window", [P, 2 * S], F32, PACK)
        b_window = tiles("b_window", [P, 2 * S], F32, PACK - 1)
        b_window.insert(2, shared.tile([P, PACK * S], F32, name="b_third", offset=0))
        a_sb = [w[:, 0:S] for w in a_window]
        b_sb = [w[:, 0:S] for w in b_window]
        b2_sb = [shared.tile([P, S], F32, name="b2_sb%d" % t, offset=4 * S * t) for t in range(PACK - 1)]
        b2_sb.append(tile("b2_last", [P, S], F32))
        a2_all = shared.tile([P, PACK, S], F32, name="a2_all", offset=4 * S * (PACK - 1))
        near_term = [t[:] for t in tiles("near_term", [P, S], F32, PACK - 1)]
        near_term.append(late.tile([P, S], F32, name="near_last", offset=1024, align_bytes=64)[:])
        b2_all = tile("b2_all", [P, PACK, S], F32)
        z_bf = [tile(name, [P, PACK * (c1 - c0)], BF16) for name, (c0, c1) in zip(("z_first", "z_mid", "z_last"), CHUNKS)]
        z_codes = tile("z_codes", [P, S], U32)
        z_scales = tile("z_scales", [P, S], U8)

        def load_weight(raw, w):
            nc.sync.dma_start(out=raw[:], in_=w.rearrange("(p j) c -> p j c", j=PACK))

        nc.vector.memset(xs[:].bitcast(I32), 0)
        load_weight(w1_raw, w1)
        nc.sync.dma_start(offs_sb[:], offs)
        for q in range(4):
            nc.sync.dma_start(
                out=xs[32 * q : 32 * q + 4, :].bitcast(I32), in_=x_scales[0, 4 * q : 4 * q + 4, :].bitcast(I32)
            )
        nc.sync.dma_start(out=xw[:], in_=x_words[0].rearrange("p n t -> p (n t)").bitcast(I32))
        load_weight(w2_raw[0], w2[:, 0:HALF])
        load_weight(w2_raw[1], w2[:, HALF:H])
        load_weight(w3_raw[0], w3[:, 0:HALF])
        load_weight(w3_raw[1], w3[:, HALF:N])
        nc.sync.dma_start(near_sb[:], near)
        nc.sync.dma_start(far_sb[:], far)

        def cast_dealt(values, raw, m0, t0, t1):
            dst = values[:].rearrange("p (t m j) -> p m j t", t=PACK, j=PACK)
            src = raw[:].rearrange("p j (m t) -> p m j t", t=PACK)
            nc.vector.tensor_copy(dst[:, m0 : m0 + src.shape[1], :, t0:t1], src[:, :, :, t0:t1])

        def quantize(codes, scales, c0, c1, values):
            nc.vector.quantize_mx(out=codes[:, c0:c1].bitcast(FP8X4), scales=scales[:, c0:c1], in_=values)

        def product(acc, i, tile_no, codes, scales):
            cols = slice(P * tile_no, P * (tile_no + 1))
            held = w_codes[3] if i == 2 and tile_no >= 2 else w_codes[i]
            nc.tensor.matmul_mx(
                out=acc,
                lhsT=held[:, cols].bitcast(FP8X4),
                lhsT_scale=w_scales[i][:, cols],
                rhs=codes.bitcast(FP8X4),
                rhs_scale=scales,
                start=True,
                stop=True,
            )

        def first_product(i, t, bank):
            acc = psum.tile([P, S], F32, name="bank%d" % bank)
            product(acc[:], i, t, xw_pick[:], xs_pick[:])
            return acc

        def offsets(lst, c0, c1):
            return lst[:, c0 // GROUP : c1 // GROUP]

        w1_bf, w2_bf = tiles("w_bf", [P, PACK * H], BF16, 2)
        cast_dealt(w1_bf, w1_raw, 0, 0, 2)
        cast_dealt(w1_bf, w1_raw, 0, 2, PACK)
        quantize(w_codes[0], w_scales[0], 0, 2 * P, w1_bf[:, 0 : 2 * H])
        quantize(w_codes[0], w_scales[0], 2 * P, H, w1_bf[:, 2 * H : PACK * H])
        nc.vector.tensor_copy(xs_pick[:], xs[:].indirect(offs_sb[:]))
        for c0 in (0, HALF):
            nc.vector.tensor_copy(xw_pick[:, c0 : c0 + HALF], xw[:].bitcast(U32).indirect(offsets(offs_sb, c0, c0 + HALF)))
        pieces = [(t, c0, c0 + HALF) for c0 in (0, HALF) for t in (0, 1)] + [(t, 0, S) for t in (2, 3)]
        for bank, (t, c0, c1) in enumerate(pieces):
            acc = psum.tile([P, c1 - c0], F32, name="bank%d" % bank)
            product(acc[:], 0, t, xw_pick[:, c0:c1], xs_pick[:, c0:c1])
            nc.scalar.activation(a_sb[t][:, c0:c1], acc[:], SIGMOID)

        cast_dealt(w2_bf, w2_raw[0], 0, 0, 2)
        cast_dealt(w2_bf, w2_raw[0], 0, 2, PACK)
        cast_dealt(w2_bf, w2_raw[1], HALF // PACK, 0, 2)
        cast_dealt(w2_bf, w2_raw[1], HALF // PACK, 2, PACK)
        quantize(w_codes[1], w_scales[1], 0, P, w2_bf[:, 0:H])
        quantize(w_codes[1], w_scales[1], P, H, w2_bf[:, H : PACK * H])
        b_ps = [first_product(1, t, (6 + t) % 8) for t in range(PACK)]

        def cast_w3(w3_bf, h, c0, c1, copy):
            copy(
                w3_bf[:, PACK * c0 : PACK * c1].rearrange("p (c i j) -> p c j i", i=2, j=PACK),
                w3_raw[h][:, :, c0:c1].rearrange("p j (c i) -> p c j i", i=2),
            )

        w3_bf = tiles("w3_bf", [P, PACK * HALF], BF16, 2)
        for h in range(2):
            cast_w3(w3_bf[h], h, 0, HALF, nc.vector.tensor_copy)
        quantize(w_codes[2], w_scales[2], 0, HALF, w3_bf[0][:])
        for t in range(PACK):
            nc.scalar.copy(b_sb[t], b_ps[t][:])

        a_near = [tile(name, [P, S], F32)[:] for name in ("w_codes1", "w_scales1", "xw_pick", "xs_pick")]
        for t in range(PACK - 1):
            nc.scalar.activation(a_near[t], a_window[t][:].indirect(near_sb[:]), COPY)
        nc.scalar.activation(a_near[3][:, 0:HALF], a_window[3][:].indirect(offsets(near_sb, 0, HALF)), COPY)

        def near_gather(t):
            nc.vector.tensor_tensor(near_term[t], b_window[t][:].indirect(near_sb[:]), a_sb[t], MULT)

        def near_sum(t):
            nc.vector.tensor_tensor(b2_sb[t][:], b_ps[t][:], near_term[t], ADD)
            first = HALF if t == PACK - 1 else 0
            nc.sync.dma_start(out=b2_all[:, t, first:S], in_=b2_sb[t][:, first:S])

        def decay_product(t, engine):
            engine.tensor_tensor(a2_all[:, t, :], a_sb[t], a_near[t], MULT)

        for t in range(PACK):
            near_gather(t)
        for t in range(2):
            decay_product(t, nc.gpsimd)
        for t in range(PACK):
            near_sum(t)
        nc.vector.tensor_tensor(b2_all[:, 3, 0:HALF], b_ps[3][:, 0:HALF], near_term[3][:, 0:HALF], ADD)
        decay_product(2, nc.vector)
        nc.vector.tensor_tensor(a2_all[:, 3, 0:HALF], a_sb[3][:, 0:HALF], a_near[3][:, 0:HALF], MULT)

        b2_far_head = tile("b2_far_head", [P, PACK, HALF], F32)
        b2_far = [b2_far_head[:], late.tile([P, PACK, P], F32, name="b2_far_mid", offset=2048, align_bytes=64)[:]]
        far_term_head = late.tile([P, PACK, HALF], F32, name="far_term_head", offset=4096, align_bytes=64)
        far_term_tail = late.tile([P, PACK, P], F32, name="far_term_tail", offset=4096, align_bytes=64)
        far_term = [far_term_head[:], tile("far_term_mid", [P, PACK, P], F32)[:], far_term_tail[:]]

        def far_gather(n):
            c0, c1 = CHUNKS[n]
            for t in range(PACK):
                nc.scalar.activation(b2_far[n][:, t, :], b2_sb[t][:].indirect(offsets(far_sb, c0, c1)), COPY)

        def far_product(n, t0=0, t1=PACK):
            c0, c1 = CHUNKS[n]
            nc.vector.tensor_tensor(far_term[n][:, t0:t1, :], b2_far[n][:, t0:t1, :], a2_all[:, t0:t1, c0:c1], MULT)

        def far_sum(n):
            c0, c1 = CHUNKS[n]
            nc.vector.tensor_tensor(
                z_bf[n][:].rearrange("p (c i t) -> p c t i", i=2, t=PACK),
                far_term[n].rearrange("p t (c i) -> p c t i", i=2),
                b2_all[:, :, c0:c1].rearrange("p t (c i) -> p c t i", i=2),
                ADD,
            )

        def quantize_z(n):
            c0, c1 = CHUNKS[n]
            quantize(z_codes, z_scales, c0, c1, z_bf[n][:])

        out_rows = out.rearrange("(r p) s -> p r s", p=P)

        def last_product(n, first_bank, rows_per_bank, last_copy=nc.scalar.copy):
            c0, c1 = CHUNKS[n]
            res = keep.tile([P, PACK, c1 - c0], F32, name="res%d" % n)
            for r0 in range(0, PACK, rows_per_bank):
                acc = psum.tile([P, rows_per_bank, c1 - c0], F32, name="bank%d" % (first_bank + r0 // rows_per_bank))
                for r in range(rows_per_bank):
                    product(acc[:, r, :], 2, r0 + r, z_codes[:, c0:c1], z_scales[:, c0:c1])
                rows = slice(r0, r0 + rows_per_bank)
                if rows.stop == PACK and last_copy is None:
                    return res, rows, acc
                nc.scalar.copy(res[:, rows, :], acc[:])
                nc.sync.dma_start(out=out_rows[:, rows, c0:c1], in_=res[:, rows, :])

        def last_chunk(n, banks):
            c0, c1 = CHUNKS[n]
            res = tiles("res_last", [P, 2, c1 - c0], F32, 2)
            for r in range(PACK):
                acc = psum.tile([P, c1 - c0], F32, name="bank%d" % banks[r])
                product(acc[:], 2, r, z_codes[:, c0:c1], z_scales[:, c0:c1])
                copy = nc.scalar.copy if r % 2 else nc.vector.tensor_copy
                copy(res[r // 2][:, r % 2, :], acc[:])
                if r % 2:
                    queue = nc.scalar if r == PACK - 1 else nc.sync
                    queue.dma_start(out=out_rows[:, r - 1 : r + 1, c0:c1], in_=res[r // 2][:])

        far_gather(0)
        a_near_late = late.tile([P, HALF], F32, name="a_near_late", offset=1024, align_bytes=64)
        nc.scalar.activation(a_near_late[:], a_window[3][:].indirect(offsets(near_sb, HALF, S)), COPY)
        far_gather(1)
        far_product(0, 0, 2)
        w_codes.append(tile("xw_pick", [P, N], U32))
        quantize(w_codes[3], w_scales[2], HALF, N, w3_bf[1][:])
        far_product(0, 2, PACK)
        b2_far.append(tile("b2_far_head", [P, PACK, P], F32)[:])
        far_gather(2)
        nc.vector.tensor_tensor(a2_all[:, 3, HALF:S], a_sb[3][:, HALF:S], a_near_late[:], MULT)
        far_sum(0)
        far_product(1)
        quantize_z(0)
        last_product(0, 2, 1)
        far_sum(1)
        far_product(2)
        quantize_z(1)
        res, rows, acc = last_product(1, 6, 2, None)
        far_sum(2)
        quantize_z(2)
        res = tile("z_last", [P, 2, P], F32)
        nc.vector.tensor_copy(res[:], acc[:])
        nc.sync.dma_start(out=out_rows[:, rows, CHUNKS[1][0] : CHUNKS[1][1]], in_=res[:])
        last_chunk(2, (0, 1, 2, 3))
